import numpy as np, ml_dtypes
CORES = [5,29,101,125,133,157,229,253]
N = 8
BF = ml_dtypes.bfloat16
S, SL, W, LN, CAP, T = 2, 1024, 2048, 3, 160, 4
def parts(rng):
    x = rng.integers(0, 256, (N, 8, 16, W)); ga = rng.integers(0, 4, (N, 8, 16, 16)); ha = rng.integers(0, 4, (N, 8, 16, 16))
    w = rng.integers(0, 256, (N, 8, 16)) << rng.integers(0, 5, (N, 8, 16)); od = rng.integers(0, 16, (N, 8))
    np.put_along_axis(w, od[:, :, None], 2 * rng.integers(0, 128, (N, 8, 1)) + 1, 2)
    return x, ga, ha, w, od
def pack(x, ga, ha, w):
    def full(b):
        z = np.zeros((N, 8, 16, 8, 16), np.float32)
        for g in range(8): z[:, g, :, g, :] = b[:, g]
        return z.reshape(N, 128, 128).astype(BF)
    return {"m": np.ascontiguousarray(x.reshape(N, 128, W)).astype(np.float32).astype(BF), "gm": full(ga), "hm": full(ha), "kw": w.reshape(N, 128, 1).astype(np.float32).astype(BF)}
def steer(x, w, i, q, g, cols, who):
    b = x[q, g][:, cols].copy(); b[i] -= b[i] & (N - 1)
    b[i] += (w[q, g, i] * (who - np.dot(w[q, g], b))) & (N - 1)
    x[q, g][:, cols] = b
def nail(x, w, i, k, q, g, cols, goal):
    b = x[q, g][:, cols].copy(); b[i] = 0; b[k] = 0
    v = (goal - np.dot(w[q, g], b)) & 65535; b[i] = v & 255; b[k] = v >> 8
    x[q, g][:, cols] = b
def still(o, q, g, ga, ha, w):
    w[q, g, o[8:]] = 0; ga[q, g][:, o[:8]] = 0; ha[q, g][:, o[:8]] = 0
def setup_inputs(rng):
    x, ga, ha, w, od = parts(rng)
    for q in range(N):
        for g in range(8):
            n = int(rng.integers(0, SL + 1)); steer(x, w, od[q, g], q, g, W - SL + rng.permutation(SL)[:n], int(rng.integers(0, N)))
        g = int(rng.integers(0, 8)); w[q, g] -= w[q, g] & 1
    return pack(x, ga, ha, w)
def setup_inputs_room(rng):
    x, ga, ha, w, od = parts(rng)
    for q in range(N):
        for g in range(8):
            if g % 2 == 0:
                o = rng.permutation(16); od[q, g] = o[0]; w[q, g, o[0]] = 2 * rng.integers(0, 128) + 1; still(o, q, g, ga, ha, w)
            for s in range(S):
                other = (q + 1 + rng.permutation(N - 1)) % N
                if q == 0: other = np.concatenate([np.array([1]), other[other != 1]])
                who = np.full(SL, q); at = 0
                for d in range(N - 1):
                    n = int(rng.choice(np.array([0, 1, CAP - 1, CAP, CAP + 1, CAP, CAP + 1, SL])))
                    if q == 0 and d == 0: n = (CAP, CAP + 1, SL, CAP - 1, CAP + 1, 0, 1, CAP)[g]
                    n = min(n, SL - at); who[at:at + n] = other[d]; at += n
                steer(x, w, od[q, g], q, g, s * SL + rng.permutation(SL), who)
    return pack(x, ga, ha, w)
def setup_inputs_full(rng):
    x, ga, ha, w, od = parts(rng); z = int(rng.integers(0, N)); p = rng.permutation(N)
    for q in range(N):
        for g in range(8):
            o = rng.permutation(16); od[q, g] = o[0]; w[q, g, o[0]] = 2 * rng.integers(0, 128) + 1; still(o, q, g, ga, ha, w)
            for s in range(S):
                if s == S - 1:
                    other = (q + 1 + rng.permutation(N - 1)) % N
                    if q != z: other = np.concatenate([np.array([z]), other[other != z]])
                    who = rng.permutation(np.repeat(other, CAP)[:SL]); who = np.concatenate([who, np.full(SL - len(who), q)])
                elif (p[q] + s) % 2 == 0: who = np.full(SL, q)
                else: who = np.full(SL, (q + int(rng.integers(1, N))) % N)
                steer(x, w, od[q, g], q, g, s * SL + np.arange(SL), who)
    return pack(x, ga, ha, w)
def setup_inputs_alike(rng):
    x, ga, ha, w, od = parts(rng); j = np.arange(SL)
    for q in range(N):
        for g in range(8):
            o = rng.permutation(16); w[q, g, o[0]] = 1; w[q, g, o[1]] = 256
            if g % 2 == 1: still(o, q, g, ga, ha, w)
            for s in range(S):
                cols = s * SL + j; nx = (s + 1) % S
                if g < 2: goal = rng.choice(np.array([0, N * W - 1, q, (W - 1) * N + q, int(rng.integers(0, N * W)), int(rng.integers(0, N * W))]), SL)
                elif g < 4: goal = (nx * SL + np.where(rng.random(SL) < 0.5, j, SL - 1 - j)) * N + np.where(rng.random(SL) < 0.3, q, rng.integers(0, N, SL))
                elif g < 6: goal = (s * SL + j) * N + rng.integers(0, N, SL)
                else: goal = np.full(SL, int(rng.integers(0, W)) * N + (q + 1) % N)
                if g == 6: x[q, g][:, cols] = x[q, g][:, s * SL:s * SL + 1]
                nail(x, w, o[0], o[1], q, g, cols, goal)
    return pack(x, ga, ha, w)
def setup_inputs_ends(rng):
    x, ga, ha, w, od = parts(rng)
    for q in range(N):
        z = rng.permutation(8)
        w[q, z[0]] = 0
        w[q, z[1]] = 4080; x[q, z[1]] = 255; ga[q, z[1]] = 3; ha[q, z[1]] = 3
        x[q, z[2]] = 0
        ga[q, z[3]] = 0; ha[q, z[3]] = 0
        ga[q, z[4]] = 0; ha[q, z[4]] = np.eye(16, dtype=np.int64)
        x[q, z[5]] = 255 * rng.integers(0, 2, (16, W)); ga[q, z[5]] = 3 * rng.integers(0, 2, (16, 16)); ha[q, z[5]] = 3 * rng.integers(0, 2, (16, 16))
        w[q, z[6]] = 0; w[q, z[6], od[q, z[6]]] = 1; ga[q, z[6]] = 3; ha[q, z[6]] = 3
        o = rng.permutation(16); big = o[:14]; g = int(z[7])
        w[q, g, big] = 16 * rng.integers(188, 256, 14); w[q, g, o[14:]] = 2 * rng.integers(0, 128, 2) + 1
        x[q, g] = rng.integers(200, 256, (16, W)); ga[q, g][:, big] = 0; ha[q, g][:, big] = 0
    return pack(x, ga, ha, w)
def setup_inputs_spread(rng):
    x, ga, ha, w, od = parts(rng)
    x = np.minimum((np.exp2(8 * rng.random((N, 8, 1, W))) * rng.random((N, 8, 16, W))).astype(np.int64), 255)
    w = (rng.integers(0, 256, w.shape) >> rng.integers(0, 8, w.shape)) << rng.integers(0, 5, w.shape)
    np.put_along_axis(w, od[:, :, None], 2 * rng.integers(0, 128, (N, 8, 1)) + 1, 2)
    ga = np.where(rng.random(ga.shape) < 0.1 + 0.9 * rng.random((N, 8, 1, 1)), ga, 0); ha = np.where(rng.random(ha.shape) < 0.1 + 0.9 * rng.random((N, 8, 1, 1)), ha, 0)
    return pack(x, ga, ha, w)
def check_inputs(d):
    bad = []
    for k, hi in (("m", 255), ("gm", 3), ("hm", 3), ("kw", 4080)):
        v = np.asarray(d[k]).astype(np.float64)
        if not np.all((v >= 0) & (v <= hi) & (v == np.floor(v))): bad.append("range of " + k)
    p = np.arange(128) >> 4; off = p[:, None] != p[None, :]
    for k in ("gm", "hm"):
        if np.any(np.asarray(d[k]).astype(np.float64)[:, off] != 0): bad.append("blocks of " + k)
    return bad
def reference(m, gm, hm, kw):
    x = m.astype(np.float32).astype(np.int64).reshape(N, 8, 16, W); w = kw.astype(np.float32).astype(np.int64).reshape(N, 8, 16, 1)
    gt = np.swapaxes(gm.astype(np.float64), 1, 2); ht = np.swapaxes(hm.astype(np.float64), 1, 2)
    me = np.eye(N, dtype=bool)[:, None, :, None]; gi = np.arange(8)[None, :, None]
    for t in range(T):
        s = t % S; lo = s * SL; pl = ((s + S - 1) % S) * SL
        prev = x[..., pl:pl + SL]; a = np.add.reduce(prev * w, axis=2)
        who = a & (N - 1); blk = (a >> LN) & (W - 1)
        h = who[:, :, None, :] == np.arange(N)[None, None, :, None]
        cnt = np.add.accumulate(h.astype(np.int64), axis=3)
        ok = np.any(h & ((cnt <= CAP) | me), axis=2)
        ref = np.swapaxes(x[who, gi, :, blk], 2, 3) * ok[:, :, None, :]
        new = np.matmul(gt, prev.reshape(N, 128, SL).astype(np.float64)) + np.matmul(ht, ref.reshape(N, 128, SL).astype(np.float64))
        x[..., lo:lo + SL] = (new.astype(np.int64).reshape(N, 8, 16, SL) + x[..., lo:lo + SL]) & 255
    return {"y": x.reshape(N, 128, W).astype(np.float32).astype(BF)}

@@ -1,0 +1,388 @@
+from concourse.bass import DstId, RemoteDMATransfer
+from concourse.mybir import AluOpType as A, ActivationFunctionType as F
+
+N, SL, WB, CAP, WAVES = 8, 1024, 2048, 160, 4
+ZC = 4 * WB
+BIG = 2048
+
+SCRATCH = {
+    "dp": ("dram", [8, 128, 64], "bfloat16"), "lp": ("dram", [8, 128, 64], "bfloat16"),
+    "d1": ("dram", [8, 128, 128], "bfloat16"), "l1": ("dram", [8, 128, 128], "bfloat16"),
+    "d0": ("dram", [8, 128, 128], "bfloat16"), "l0": ("dram", [8, 128, 128], "bfloat16"),
+    "ya": ("dram", [8, 128, 128], "bfloat16"), "yb": ("dram", [8, 128, 128], "bfloat16"),
+    "win": ("sbuf", [128, ZC + 16], "bfloat16"),
+    "ref": ("sbuf", [128, 2048], "bfloat16"),
+    "tq": ("sbuf", [128, SL], "bfloat16"),
+    "off": ("sbuf", [128, 128], "uint16"),
+    "ai": ("sbuf", [128, 128], "int32"), "who": ("sbuf", [128, 128], "int32"), "blk": ("sbuf", [128, 128], "int32"),
+    "blkf": ("sbuf", [128, 128], "float32"),
+    "hot": ("sbuf", [128, 512], "bfloat16"), "run": ("sbuf", [128, 512], "bfloat16"), "okk": ("sbuf", [128, 512], "bfloat16"),
+    "keep": ("sbuf", [128, 512], "bfloat16"), "ones": ("sbuf", [128, 512], "bfloat16"),
+    "jj": ("sbuf", [128, 128], "int32"), "pp": ("sbuf", [128, 8], "int32"),
+    "ti": ("sbuf", [128, 384], "int32"), "tk": ("sbuf", [128, 256], "float32"),
+    "ci": ("sbuf", [128, 16], "int32"), "cf": ("sbuf", [128, 16], "float32"), "cg": ("sbuf", [128, 8], "float32"),
+    "sli": ("sbuf", [128, 8], "int32"), "slf": ("sbuf", [128, 4], "float32"), "grp": ("sbuf", [128, 8], "float32"),
+    "id2": ("sbuf", [128, 256], "bfloat16"), "idf": ("sbuf", [128, 128], "float32"),
+    "coef": ("sbuf", [128, 512], "bfloat16"), "one8": ("sbuf", [128, 128], "bfloat16"),
+    "low": ("sbuf", [128, 256], "bfloat16"), "upp": ("sbuf", [128, 128], "bfloat16"), "swp": ("sbuf", [128, 128], "bfloat16"),
+    "msk": ("sbuf", [128, 1024], "bfloat16"), "lw": ("sbuf", [128, 1024], "bfloat16"), "c258": ("sbuf", [128, 128], "bfloat16"),
+    "wc": ("sbuf", [128, 16], "bfloat16"), "gcb": ("sbuf", [128, 16], "bfloat16"), "hc": ("sbuf", [128, 16], "bfloat16"),
+    "gbd": ("sbuf", [128, 128], "bfloat16"), "hb": ("sbuf", [128, 256], "bfloat16"), "hl": ("sbuf", [128, 256], "bfloat16"),
+    "p0a": ("psum", [128, 512], "float32"), "p0b": ("psum", [128, 512], "float32"),
+    "p1a": ("psum", [128, 512], "float32"), "p1b": ("psum", [128, 512], "float32"),
+    "pa": ("psum", [128, 512], "float32"), "pc": ("psum", [128, 512], "float32"),
+    "r0": ("psum", [128, 512], "float32"), "r1": ("psum", [128, 512], "float32"),
+}
+SEMAPHORES = (["iot", "cv", "st0", "st1", "st2", "st3", "st4", "ar0", "ar1", "ar2", "ar3", "ar4", "sin", "sout",
+               "ldw", "ldg", "ldx1", "ldx0", "repd", "slw", "bd", "hs", "shl", "sa", "v1", "v2", "v3", "v4", "v5", "v6",
+               "sc", "v7", "ss", "v8", "ph0", "ph1", "q0", "q1", "n0", "n1", "fin"]
+              + ["ga%d" % i for i in range(4)] + ["pr%d" % i for i in range(6)] + ["ev%d" % i for i in range(6)])
+SRC = ["dp", "d1", "d0", "d0", "d1"]
+DST = ["lp", "l1", "l0", "ya", "yb"]
+STAGED = [80, 16, 16, 32, 32]
+
+
+def bits(engines):
+    m = 0
+    for e in engines:
+        m |= 1 << e
+    return m
+
+
+def routes(T, topo, r):
+    src = T.cores[r]
+    near = [q for q in range(N) if q != r and topo.may_write(src, T.cores[q])]
+    far = [q for q in range(N) if q != r and q not in near]
+    able = [h for h in topo.cores_of(src) if h != src and all(topo.may_write(h, T.cores[q]) for q in far)]
+    able.sort(key=lambda h: (topo.die(h) == topo.die(src), h))
+    me = sorted(near + [r]).index(r)
+    return near, [(able[(me + b) % len(able)], q) for b, q in enumerate(far)], able
+
+
+def helper_program(g, core, T, topo):
+    for r in range(N):
+        near, far, able = routes(T, topo, r)
+        for h, q in far:
+            if h != core:
+                continue
+            dst = T.cores[q]
+            rid, pid = topo.addr(dst, core)
+            eng = topo.engines(core, dst)[0::2]
+            for k in range(5):
+                g.wait_ge(T.sem["ar%d" % k], 2)
+                g.remote_dma(T[DST[k]][r], T[DST[k]][0], T.sem["ar%d" % k], T.sem.sin, pid, rid, bits(eng))
+            g.wait_ge(T.sem.sin, 5 * len(eng))
+
+
+def rank_program(g, core, T, topo):
+    me = T.rank_of(core)
+    if me is None:
+        helper_program(g, core, T, topo)
+        return
+    V, P, S, Y = g.vector, g.tensor, g.scalar, g.sync
+    cnt, seen = {}, {}
+
+    def inc(ins, name, n=1):
+        ins.then_inc(T.sem[name], n)
+        cnt[name] = cnt.get(name, 0) + n
+
+    def wait(q, name, n):
+        q.wait_ge(T.sem[name], n)
+        seen[name] = max(seen.get(name, 0), n)
+
+    near, far, able = routes(T, topo, me)
+    off_eng = topo.engines(core, T.cores[near[0]])
+    on_eng = [e for e in topo.engines(core, able[0]) if e not in off_eng]
+    hmask = {}
+    for x, h in enumerate(able):
+        b = 4 * (x % 2) + x // 2
+        hmask[h] = bits([on_eng[b], on_eng[b + 2]])
+    sent = len(near) + 2 * len(far)
+    come = 16 + len(near) + len(far) * len(off_eng[0::2])
+
+    def send(k, lsem):
+        out = []
+        for h, q in far:
+            rid, pid = topo.addr(h, core)
+            out.append(RemoteDMATransfer(dst_ids=[DstId(rid=rid, pnc=pid)], dma_engine_mask=hmask[h],
+                                         remote_sem=T.sem["ar%d" % k], src=T[SRC[k]][q], dst=T[DST[k]][0]))
+        for x, q in enumerate(near):
+            rid, pid = topo.addr(T.cores[q], core)
+            out.append(RemoteDMATransfer(dst_ids=[DstId(rid=rid, pnc=pid)], dma_engine_mask=bits([off_eng[2 * x]]),
+                                         remote_sem=T.sem["ar%d" % k], src=T[SRC[k]][q], dst=T[DST[k]][me]))
+        g.remote_dma_fused(out, local_sem=T.sem[lsem])
+
+    def own(k):
+        Y.dma_start(T[DST[k]][me], T[SRC[k]][me]).then_inc(T.sem["ar%d" % k], 16)
+
+    W = T.win
+
+    def cols(sg, s, h=None):
+        a = sg * WB + s * SL
+        return slice(a, a + SL) if h is None else slice(a + 512 * h, a + 512 * h + 512)
+
+    Y.dma_start(T.dp[:, 64, 0:16], T.kw[:]).then_inc(T.sem.st0, 16)
+    Y.dma_start(T.dp[:, 64, 16:64], T.m[:, 0:3]).then_inc(T.sem.st0, 16)
+    Y.dma_start(T.dp[:, 65:128, :], T.m[:, 0:252]).then_inc(T.sem.st0, 16)
+    S.dma_start(T.dp[:, 0:32, :], T.gm[:]).then_inc(T.sem.st0, 16)
+    S.dma_start(T.dp[:, 32:64, :], T.hm[:]).then_inc(T.sem.st0, 16)
+    S.dma_start(T.d1[:], T.m[:, SL:WB]).then_inc(T.sem.st1, 16)
+    Y.dma_start(T.d0[:], T.m[:, 0:SL]).then_inc(T.sem.st2, 16)
+
+    inc(g.iota(T.jj[:], [[1, 128]], 0, 0), "iot")
+    inc(g.iota(T.pp[:], [[0, 8]], 0, 1), "iot")
+    for k, n in enumerate(STAGED):
+        g.wait_ge(T.sem["st%d" % k], n)
+        send(k, "sin" if k < 3 else "sout")
+    g.wait_ge(T.sem.sout, 2 * sent)
+
+    def level():
+        wait(V, "cv", cnt["cv"])
+
+    def ts(out, in0, s1, op0, s2=None, op1=None):
+        if op1 is None:
+            return V.tensor_scalar(out, in0, s1, None, op0)
+        return V.tensor_scalar(out, in0, s1, s2, op0, op1)
+
+    inc(V.memset(T.ones[:], 1.0), "cv")
+    inc(V.memset(T.keep[:], 1.0), "cv")
+    inc(V.memset(T.c258[:], 258.0), "cv")
+    inc(V.memset(T.hb[:], 0.0), "cv")
+    inc(V.memset(W[:, ZC:ZC + 16], 0.0), "cv")
+    wait(V, "iot", 2)
+    sr, an = A.logical_shift_right, A.bitwise_and
+    J, pc0 = T.jj, T.pp[:, 0:1]
+    inc(ts(T.ti[:, 0:128], J[:], 3, sr), "cv")
+    inc(ts(T.ti[:, 128:256], J[:], 5, sr), "cv")
+    inc(ts(T.ti[:, 256:384], J[:], 15, an), "cv")
+    inc(V.tensor_copy(T.ci[:, 0:1], pc0), "cv")
+    inc(ts(T.ci[:, 1:2], pc0, 3, sr), "cv")
+    inc(ts(T.ci[:, 2:3], pc0, 4, sr), "cv")
+    inc(ts(T.ci[:, 3:4], pc0, 5, sr), "cv")
+    inc(ts(T.ci[:, 4:5], pc0, 15, an), "cv")
+    inc(ts(T.ci[:, 5:6], pc0, 4, sr, 1, an), "cv")
+    inc(ts(T.ci[:, 6:7], pc0, 3, sr, 1, an), "cv")
+    level()
+    inc(V.tensor_copy(T.cf[:, 0:7], T.ci[:, 0:7]), "cv")
+    inc(ts(T.tk[:, 0:128], T.ti[:, 128:256], 16.0, A.mult), "cv")
+    level()
+    cf = T.cf
+    inc(V.tensor_tensor(T.tk[:, 128:256], T.tk[:, 0:128], T.ti[:, 256:384], A.add), "cv")
+    inc(ts(T.cg[:, 0:1], cf[:, 3:4], 16.0, A.mult, cf[:, 4:5], A.add), "cv")
+    inc(ts(T.cg[:, 1:2], cf[:, 3:4], 2.0, A.mult, cf[:, 5:6], A.add), "cv")
+    inc(V.tensor_tensor(T.cg[:, 3:4], cf[:, 5:6], cf[:, 6:7], A.not_equal), "cv")
+    inc(ts(T.sli[:, 0:4], J[:, 0:4], 2.0, A.mult, cf[:, 2:3], A.add), "cv")
+    inc(ts(T.grp[:], J[:, 0:8], cf[:, 2:3], A.is_equal), "cv")
+    inc(ts(T.id2[:, 0:128], J[:], cf[:, 0:1], A.is_equal), "cv")
+    inc(ts(T.id2[:, 128:256], J[:], cf[:, 0:1], A.is_equal), "cv")
+    inc(ts(T.idf[:], J[:], cf[:, 0:1], A.is_equal), "cv")
+    for sg in range(4):
+        inc(ts(T.coef[:, 128 * sg:128 * sg + 128], J[:], cf[:, 0:1], A.is_equal, float(sg * WB - ZC), A.mult), "cv")
+    inc(ts(T.one8[:], T.ti[:, 0:128], cf[:, 1:2], A.is_equal), "cv")
+    inc(ts(T.low[:, 0:128], J[:], cf[:, 0:1], A.is_lt, -1.0, A.mult), "cv")
+    level()
+    inc(ts(T.cg[:, 2:3], T.cg[:, 1:2], 8.0, A.mult), "cv")
+    inc(ts(T.sli[:, 4:8], T.sli[:, 0:4], 7, an), "cv")
+    inc(V.tensor_tensor(T.low[:, 128:256], T.low[:, 0:128], T.one8[:], A.mult), "cv")
+    inc(ts(T.swp[:], T.tk[:, 128:256], T.cg[:, 0:1], A.is_equal), "cv")
+    inc(ts(T.keep[:, 0:128], T.ones[:, 0:128], T.cg[:, 3:4], A.mult), "cv")
+    level()
+    inc(V.tensor_copy(T.slf[:], T.sli[:, 4:8]), "cv")
+    inc(V.tensor_tensor(T.upp[:], T.low[:, 128:256], T.coef[:, 384:512], A.add), "cv")
+    inc(V.memset(T.keep[:, 0:512:128], 0.0), "cv")
+    for e in range(8):
+        inc(ts(T.msk[:, 128 * e:128 * e + 128], T.tk[:, 128:256], float(e), A.subtract, T.cg[:, 2:3], A.is_equal), "cv")
+    level()
+    consts = cnt["cv"]
+    wait(V, "ldw", 16)
+    inc(ts(T.lw[:], T.msk[:], T.wc[:, 0:1], A.mult), "slw")
+
+    for k in range(3):
+        Y.wait_ge(T.sem["st%d" % k], STAGED[k])
+        own(k)
+
+    def turned(sg, s, src):
+        inc(Y.dma_start(W[0:128 - 32 * sg, cols(sg, s)], src[2 * sg:8]), "repd", 16)
+        inc(Y.dma_start(W[128 - 32 * sg:128, cols(sg, s)], src[0:2 * sg]), "repd", 16)
+
+    Y.wait_ge(T.sem.ar0, come)
+    inc(Y.dma_start(T.wc[:, 0:1], T.lp[:, 64, 0:16]), "ldw", 16)
+    Y.wait_ge(T.sem.ar1, come)
+    inc(Y.dma_start(W[:, cols(0, 1)], T.l1[:]), "ldx1", 16)
+    turned(2, 1, T.l1)
+    Y.wait_ge(T.sem.ar2, come)
+    inc(Y.dma_start(W[:, cols(0, 0)], T.l0[:]), "ldx0", 16)
+    turned(2, 0, T.l0)
+    turned(1, 0, T.l0)
+
+    S.wait_ge(T.sem.ar0, come)
+    row, c0 = me // 4, (16 * me) % 64
+    inc(S.dma_start(T.gcb[:], T.lp[:, row:32:2, c0:c0 + 16]), "ldg", 16)
+    inc(S.dma_start(T.hc[:], T.lp[:, 32 + row:64:2, c0:c0 + 16]), "ldg", 16)
+    wait(S, "cv", consts)
+    wait(S, "ldg", 32)
+    for r in range(8):
+        a = 128 * (r % 2) + 16 * r
+        inc(S.activation(T.hb[:, a:a + 16], T.hc[:], F.Copy, scale=T.grp[:, r:r + 1]), "bd")
+    for r in range(8):
+        inc(S.activation(T.gbd[:, 16 * r:16 * r + 16], T.gcb[:], F.Copy, scale=T.grp[:, r:r + 1]), "bd")
+    wait(P, "cv", consts)
+
+    banks = [[T.p0a, T.p0b], [T.p1a, T.p1b]]
+    ident = T.id2[:, 0:128]
+
+    def base(t, b):
+        P.matmul(banks[t % 2][b][:], T.c258[:], T.ones[:], True, False)
+        P.matmul(banks[t % 2][b][:], ident, W[:, cols(0, t % 2, b)], False, False)
+
+    for t in range(WAVES):
+        s, sp, n = t % 2, (t + 1) % 2, t + 1
+        mine, other = banks[t % 2], banks[(t + 1) % 2]
+        jobs = [(1, sp, 0, T.r0), (3, sp, 0, other[0]), (1, sp, 1, T.r1), (3, sp, 1, other[1])]
+        if t == 0:
+            jobs += [(3, 0, 0, T.r0), (3, 0, 1, T.r1)]
+
+        def turn(x):
+            sg, sl, h, bank = jobs[x]
+            inc(P.matmul(bank[:], T.id2[:, 32 * sg:32 * sg + 128], W[:, cols(0, sl, h)], True, True), "pr%d" % x)
+
+        def evac(x):
+            sg, sl, h, bank = jobs[x]
+            wait(S, "pr%d" % x, n)
+            inc(S.activation(W[:, cols(sg, sl, h)], bank[:], F.Copy), "ev%d" % x)
+
+        def gprev(b):
+            P.matmul(mine[b][:], T.gbd[:], W[:, cols(0, sp, b)], False, False)
+
+        if t == 0:
+            wait(P, "slw", 1)
+            wait(P, "ldx1", 16)
+        else:
+            wait(P, "n0", t)
+            turn(0)
+            wait(P, "n1", t)
+        for e in range(8):
+            a = sp * SL + e
+            mm = P.matmul(T.pa[:, 0:128], T.lw[:, 128 * e:128 * e + 128], W[:, a:a + SL - e:8], e == 0, e == 7)
+        inc(mm, "sa")
+        if t == 0:
+            turn(0)
+        turn(1)
+        turn(2)
+        if t == 0:
+            wait(P, "bd", 16)
+            inc(P.matmul(T.p0a[:, 0:256], T.swp[:], T.hb[:], True, True), "hs")
+        wait(P, "v3", 4 * n)
+        P.matmul(T.pc[:], T.upp[:], T.hot[:], True, False)
+        wait(P, "v4", n)
+        inc(P.matmul(T.pc[:], T.one8[:], T.run[:], False, True), "sc")
+        turn(3)
+        if t == 0:
+            wait(P, "ldx0", 16)
+            wait(P, "ev0", 1)
+            turn(4)
+            wait(P, "ev2", 1)
+            turn(5)
+        wait(P, "v6", n)
+        P.matmul(T.pa[:, 128:256], T.idf[:], T.blkf[:], True, False)
+        if t == 0:
+            wait(P, "shl", 1)
+            base(0, 0)
+        else:
+            gprev(0)
+        wait(P, "v7", n)
+        for sg in range(4):
+            mm = P.matmul(T.pa[:, 128:256], T.coef[:, 128 * sg:128 * sg + 128], T.okk[:, 128 * sg:128 * sg + 128],
+                          False, sg == 3)
+        inc(mm, "ss")
+        if t == 0:
+            gprev(0)
+            base(0, 1)
+        gprev(1)
+        for b in range(2):
+            wait(P, "ga%d" % (2 * b), n)
+            wait(P, "ga%d" % (2 * b + 1), n)
+            for c in range(16):
+                q, e = c // 8, c % 8
+                mm = P.matmul(mine[b][:, e:512:8], T.hl[:, 128 * q:128 * q + 128], T.ref[:, SL * b + c:SL * b + SL:16],
+                              False, c == 15)
+            inc(mm, "ph%d" % b)
+        if t + 1 < WAVES:
+            base(t + 1, 0)
+            base(t + 1, 1)
+
+        if t > 0:
+            for h in range(2):
+                wait(Y, "n%d" % h, t)
+                inc(Y.dma_start(W[0:64, cols(2, sp, h)], W[64:128, cols(0, sp, h)]), "repd", 16)
+                inc(Y.dma_start(W[64:128, cols(2, sp, h)], W[0:64, cols(0, sp, h)]), "repd", 16)
+        reps = cnt["repd"]
+        if t == 3:
+            Y.wait_ge(T.sem.sin, 3 * sent)
+            for h in range(2):
+                Y.dma_start(T.d0[:, 64 * h:64 * h + 64, :], W[:, cols(0, 0, h)]).then_inc(T.sem.st3, 16)
+            Y.wait_ge(T.sem.st3, 32)
+            own(3)
+
+        for x in range(len(jobs)):
+            if t == 0 and x == 3:
+                wait(S, "hs", 1)
+                inc(S.activation(T.hl[:], T.p0a[:, 0:256], F.Copy), "shl")
+            evac(x)
+
+        def ready(q):
+            wait(q, "v8", n)
+            wait(q, "repd", reps)
+            for x in range(len(jobs)):
+                wait(q, "ev%d" % x, n)
+
+        ready(S)
+        for c in (1, 3):
+            inc(S.activation(T.ref[:, 512 * c:512 * c + 512], W[:, 0:ZC + 16].indirect(T.off[:, 32 * c:32 * c + 32]), F.Copy),
+                "ga%d" % c)
+        for b in range(2):
+            wait(S, "ph%d" % b, n)
+            inc(S.activation(T.tq[:, 512 * b:512 * b + 512], mine[b][:], F.Identity, bias=-127.5), "q%d" % b)
+
+        wait(V, "sa", n)
+        inc(V.tensor_copy(T.ai[:], T.pa[:, 0:128]), "v1")
+        wait(V, "v1", n)
+        inc(ts(T.who[:], T.ai[:], N - 1, an), "v2")
+        wait(V, "v2", n)
+        for sg in range(4):
+            inc(ts(T.hot[:, 128 * sg:128 * sg + 128], T.who[:], T.slf[:, sg:sg + 1], A.is_equal), "v3")
+        wait(V, "v3", 4 * n)
+        inc(V.tensor_tensor_scan(T.run[:], T.keep[:], T.hot[:], 0.0, A.mult, A.add), "v4")
+        inc(ts(T.blk[:], T.ai[:], 3, sr, WB - 1, an), "v5")
+        wait(V, "v5", n)
+        inc(V.tensor_copy(T.blkf[:], T.blk[:]), "v6")
+        wait(V, "sc", n)
+        inc(ts(T.okk[:], T.pc[:], float(CAP - BIG), A.is_le), "v7")
+        wait(V, "ss", n)
+        inc(ts(T.off[:], T.pa[:, 128:256], float(ZC), A.add, float(ZC), A.min), "v8")
+        ready(V)
+        for c in (0, 2):
+            inc(V.tensor_copy(T.ref[:, 512 * c:512 * c + 512], W[:, 0:ZC + 16].indirect(T.off[:, 32 * c:32 * c + 32])),
+                "ga%d" % c)
+        for c in range(4):
+            wait(V, "ga%d" % c, n)
+        for b in range(2):
+            wait(V, "q%d" % b, n)
+            inc(V.tensor_tensor(W[:, cols(0, s, b)], mine[b][:], T.tq[:, 512 * b:512 * b + 512], A.subtract), "n%d" % b)
+
+    for h in range(2):
+        wait(Y, "n%d" % h, WAVES)
+        Y.dma_start(T.d1[:, 64 * h:64 * h + 64, :], W[:, cols(0, 1, h)]).then_inc(T.sem.st4, 16)
+    Y.wait_ge(T.sem.st4, 32)
+    own(4)
+    S.wait_ge(T.sem.sout, 2 * sent)
+    S.wait_ge(T.sem.ar3, come)
+    for h in range(2):
+        S.dma_start(T.y[:, 512 * h:512 * h + 512], T.ya[:, 64 * h:64 * h + 64, :]).then_inc(T.sem.fin, 16)
+    for h, q in enumerate((Y, S)):
+        q.wait_ge(T.sem.ar4, come)
+        q.dma_start(T.y[:, SL + 512 * h:SL + 512 * h + 512], T.yb[:, 64 * h:64 * h + 64, :]).then_inc(T.sem.fin, 16)
+    Y.wait_ge(T.sem.fin, 64)
+    for name in cnt:
+        if seen.get(name, 0) < cnt[name]:
+            P.wait_ge(T.sem[name], cnt[name])

@@ -4,6 +4,7 @@ from concourse.mybir import AluOpType as A, ActivationFunctionType as F
 N, SL, WB, CAP, WAVES = 8, 1024, 2048, 160, 4
 ZC = 4 * WB
 BIG = 2048
+COEF = [float(-ZC), float(WB - ZC), (2 * WB - ZC) / 2, (3 * WB - ZC) / 2]
 
 SCRATCH = {
     "dp": ("dram", [8, 128, 64], "bfloat16"), "lp": ("dram", [8, 128, 64], "bfloat16"),
@@ -35,7 +36,7 @@ SCRATCH = {
 }
 SEMAPHORES = (["iot", "cv", "st0", "st1", "st2", "st3", "st4", "ar0", "ar1", "ar2", "ar3", "ar4", "sin", "sout",
                "ldw", "ldg", "ldx1", "ldx0", "repd", "slw", "bd", "hs", "shl", "sa", "v1", "v2", "v3", "v4", "v5", "v6",
-               "sc", "v7", "ss", "v8", "ph0", "ph1", "q0", "q1", "n0", "n1", "fin"]
+               "sc", "sc2", "v7", "s7", "ss", "v8", "ph0", "ph1", "q0", "q1", "n0", "n1", "fin"]
               + ["ga%d" % i for i in range(4)] + ["pr%d" % i for i in range(6)] + ["ev%d" % i for i in range(6)])
 SRC = ["dp", "d1", "d0", "d0", "d1"]
 DST = ["lp", "l1", "l0", "ya", "yb"]
@@ -177,7 +178,7 @@ def rank_program(g, core, T, topo):
     inc(ts(T.id2[:, 128:256], J[:], cf[:, 0:1], A.is_equal), "cv")
     inc(ts(T.idf[:], J[:], cf[:, 0:1], A.is_equal), "cv")
     for sg in range(4):
-        inc(ts(T.coef[:, 128 * sg:128 * sg + 128], J[:], cf[:, 0:1], A.is_equal, float(sg * WB - ZC), A.mult), "cv")
+        inc(ts(T.coef[:, 128 * sg:128 * sg + 128], J[:], cf[:, 0:1], A.is_equal, COEF[sg], A.mult), "cv")
     inc(ts(T.one8[:], T.ti[:, 0:128], cf[:, 1:2], A.is_equal), "cv")
     inc(ts(T.low[:, 0:128], J[:], cf[:, 0:1], A.is_lt, -1.0, A.mult), "cv")
     level()
@@ -188,7 +189,7 @@ def rank_program(g, core, T, topo):
     inc(ts(T.keep[:, 0:128], T.ones[:, 0:128], T.cg[:, 3:4], A.mult), "cv")
     level()
     inc(V.tensor_copy(T.slf[:], T.sli[:, 4:8]), "cv")
-    inc(V.tensor_tensor(T.upp[:], T.low[:, 128:256], T.coef[:, 384:512], A.add), "cv")
+    inc(V.tensor_tensor(T.upp[:], T.low[:, 128:256], T.coef[:, 256:384], A.add), "cv")
     inc(V.memset(T.keep[:, 0:512:128], 0.0), "cv")
     for e in range(8):
         inc(ts(T.msk[:, 128 * e:128 * e + 128], T.tk[:, 128:256], float(e), A.subtract, T.cg[:, 2:3], A.is_equal), "cv")
@@ -240,7 +241,7 @@ def rank_program(g, core, T, topo):
         mine, other = banks[t % 2], banks[(t + 1) % 2]
         jobs = [(1, sp, 0, T.r0), (3, sp, 0, other[0]), (1, sp, 1, T.r1), (3, sp, 1, other[1])]
         if t == 0:
-            jobs += [(3, 0, 0, T.r0), (3, 0, 1, T.r1)]
+            jobs += [(3, 0, 0, other[0]), (3, 0, 1, T.r1)]
 
         def turn(x):
             sg, sl, h, bank = jobs[x]
@@ -254,49 +255,55 @@ def rank_program(g, core, T, topo):
         def gprev(b):
             P.matmul(mine[b][:], T.gbd[:], W[:, cols(0, sp, b)], False, False)
 
+        def named(k0, k1):
+            for e in range(8):
+                a = sp * SL
+                mm = P.matmul(T.pa[:, k0:k1], T.lw[:, 128 * e:128 * e + 128], W[:, a + 8 * k0 + e:a + 8 * k1:8], e == 0, e == 7)
+            inc(mm, "sa")
+
         if t == 0:
             wait(P, "slw", 1)
             wait(P, "ldx1", 16)
+            named(0, 128)
+            turn(0)
         else:
             wait(P, "n0", t)
+            named(0, 64)
             turn(0)
             wait(P, "n1", t)
-        for e in range(8):
-            a = sp * SL + e
-            mm = P.matmul(T.pa[:, 0:128], T.lw[:, 128 * e:128 * e + 128], W[:, a:a + SL - e:8], e == 0, e == 7)
-        inc(mm, "sa")
-        if t == 0:
-            turn(0)
+            named(64, 128)
         turn(1)
         turn(2)
+        turn(3)
         if t == 0:
             wait(P, "bd", 16)
             inc(P.matmul(T.p0a[:, 0:256], T.swp[:], T.hb[:], True, True), "hs")
+        wait(P, "ev0", n)
         wait(P, "v3", 4 * n)
-        P.matmul(T.pc[:], T.upp[:], T.hot[:], True, False)
+        P.matmul(T.pc[:, 0:256], T.upp[:], T.hot[:, 0:256], True, False)
+        P.matmul(T.r0[:, 0:256], T.upp[:], T.hot[:, 256:512], True, False)
         wait(P, "v4", n)
-        inc(P.matmul(T.pc[:], T.one8[:], T.run[:], False, True), "sc")
-        turn(3)
+        inc(P.matmul(T.pc[:, 0:256], T.one8[:], T.run[:, 0:256], False, True), "sc")
+        inc(P.matmul(T.r0[:, 0:256], T.one8[:], T.run[:, 256:512], False, True), "sc2")
         if t == 0:
             wait(P, "ldx0", 16)
-            wait(P, "ev0", 1)
+            wait(P, "ev1", 1)
             turn(4)
             wait(P, "ev2", 1)
             turn(5)
         wait(P, "v6", n)
         P.matmul(T.pa[:, 128:256], T.idf[:], T.blkf[:], True, False)
-        if t == 0:
-            wait(P, "shl", 1)
-            base(0, 0)
-        else:
-            gprev(0)
-        wait(P, "v7", n)
         for sg in range(4):
+            if sg % 2 == 0:
+                wait(P, "v7" if sg == 0 else "s7", n)
             mm = P.matmul(T.pa[:, 128:256], T.coef[:, 128 * sg:128 * sg + 128], T.okk[:, 128 * sg:128 * sg + 128],
                           False, sg == 3)
         inc(mm, "ss")
         if t == 0:
-            gprev(0)
+            wait(P, "shl", 1)
+            base(0, 0)
+        gprev(0)
+        if t == 0:
             base(0, 1)
         gprev(1)
         for b in range(2):
@@ -324,17 +331,21 @@ def rank_program(g, core, T, topo):
             Y.wait_ge(T.sem.st3, 32)
             own(3)
 
-        for x in range(len(jobs)):
-            if t == 0 and x == 3:
-                wait(S, "hs", 1)
-                inc(S.activation(T.hl[:], T.p0a[:, 0:256], F.Copy), "shl")
+        for x in range(4):
             evac(x)
+        wait(S, "sc2", n)
+        inc(S.activation(T.okk[:, 256:512], T.r0[:, 0:256], F.Sign, bias=CAP - BIG + 0.5, scale=-1.0), "s7")
+        if t == 0:
+            wait(S, "hs", 1)
+            inc(S.activation(T.hl[:], T.p0a[:, 0:256], F.Copy), "shl")
+            evac(4)
+            evac(5)
 
         def ready(q):
-            wait(q, "v8", n)
             wait(q, "repd", reps)
             for x in range(len(jobs)):
                 wait(q, "ev%d" % x, n)
+            wait(q, "v8", n)
 
         ready(S)
         for c in (1, 3):
@@ -344,7 +355,7 @@ def rank_program(g, core, T, topo):
             wait(S, "ph%d" % b, n)
             inc(S.activation(T.tq[:, 512 * b:512 * b + 512], mine[b][:], F.Identity, bias=-127.5), "q%d" % b)
 
-        wait(V, "sa", n)
+        wait(V, "sa", cnt["sa"])
         inc(V.tensor_copy(T.ai[:], T.pa[:, 0:128]), "v1")
         wait(V, "v1", n)
         inc(ts(T.who[:], T.ai[:], N - 1, an), "v2")
@@ -357,9 +368,9 @@ def rank_program(g, core, T, topo):
         wait(V, "v5", n)
         inc(V.tensor_copy(T.blkf[:], T.blk[:]), "v6")
         wait(V, "sc", n)
-        inc(ts(T.okk[:], T.pc[:], float(CAP - BIG), A.is_le), "v7")
+        inc(ts(T.okk[:, 0:256], T.pc[:, 0:256], float(CAP - BIG), A.is_le), "v7")
         wait(V, "ss", n)
-        inc(ts(T.off[:], T.pa[:, 128:256], float(ZC), A.add, float(ZC), A.min), "v8")
+        inc(ts(T.off[:], T.pa[:, 128:256], ZC + COEF[2] + COEF[3], A.add, float(ZC), A.min), "v8")
         ready(V)
         for c in (0, 2):
             inc(V.tensor_copy(T.ref[:, 512 * c:512 * c + 512], W[:, 0:ZC + 16].indirect(T.off[:, 32 * c:32 * c + 32])),

@@ -10,7 +10,9 @@ SCRATCH = {
     "dp": ("dram", [8, 128, 64], "bfloat16"), "lp": ("dram", [8, 128, 64], "bfloat16"),
     "d1": ("dram", [8, 128, 128], "bfloat16"), "l1": ("dram", [8, 128, 128], "bfloat16"),
     "d0": ("dram", [8, 128, 128], "bfloat16"), "l0": ("dram", [8, 128, 128], "bfloat16"),
-    "ya": ("dram", [8, 128, 128], "bfloat16"), "yb": ("dram", [8, 128, 128], "bfloat16"),
+    "ya": ("dram", [8, 128, 128], "bfloat16"),
+    "db": ("dram", [8, 128, 64], "bfloat16"), "yb": ("dram", [8, 128, 64], "bfloat16"),
+    "yc": ("dram", [8, 128, 64], "bfloat16"),
     "win": ("sbuf", [128, ZC + 16], "bfloat16"),
     "ref": ("sbuf", [128, 2048], "bfloat16"),
     "tq": ("sbuf", [128, SL], "bfloat16"),
@@ -34,13 +36,14 @@ SCRATCH = {
     "pa": ("psum", [128, 512], "float32"), "pc": ("psum", [128, 512], "float32"),
     "r0": ("psum", [128, 512], "float32"), "r1": ("psum", [128, 512], "float32"),
 }
-SEMAPHORES = (["iot", "cv", "st0", "st1", "st2", "st3", "st4", "ar0", "ar1", "ar2", "ar3", "ar4", "sin", "sout",
-               "ldw", "ldg", "ldx1", "ldx0", "repd", "slw", "bd", "hs", "shl", "sa", "v1", "v2", "v3", "v4", "v5", "v6",
-               "sc", "sc2", "v7", "s7", "ss", "v8", "ph0", "ph1", "q0", "q1", "n0", "n1", "fin"]
+SEMAPHORES = (["iot", "cv", "sin", "sout",
+               "ldw", "ldg", "ldx1", "ldx0", "repd", "slw", "bd", "hs", "shl", "sa", "v1", "v2", "v3", "w3", "v4", "w4", "v5",
+               "v6", "sc", "sc2", "v7", "s7", "ss", "v8", "ph0", "ph1", "q0", "q1", "n0", "n1", "fin"]
+              + ["st%d" % i for i in range(6)] + ["ar%d" % i for i in range(6)]
               + ["ga%d" % i for i in range(4)] + ["pr%d" % i for i in range(6)] + ["ev%d" % i for i in range(6)])
-SRC = ["dp", "d1", "d0", "d0", "d1"]
-DST = ["lp", "l1", "l0", "ya", "yb"]
-STAGED = [80, 16, 16, 32, 32]
+SRC = ["dp", "d1", "d0", "d0", "dp", "db"]
+DST = ["lp", "l1", "l0", "ya", "yb", "yc"]
+STAGED = [80, 16, 16, 32, 16, 16]
 
 
 def bits(engines):
@@ -69,10 +72,10 @@ def helper_program(g, core, T, topo):
             dst = T.cores[q]
             rid, pid = topo.addr(dst, core)
             eng = topo.engines(core, dst)[0::2]
-            for k in range(5):
+            for k in range(len(DST)):
                 g.wait_ge(T.sem["ar%d" % k], 2)
                 g.remote_dma(T[DST[k]][r], T[DST[k]][0], T.sem["ar%d" % k], T.sem.sin, pid, rid, bits(eng))
-            g.wait_ge(T.sem.sin, 5 * len(eng))
+            g.wait_ge(T.sem.sin, len(DST) * len(eng))
 
 
 def rank_program(g, core, T, topo):
@@ -135,7 +138,7 @@ def rank_program(g, core, T, topo):
     for k, n in enumerate(STAGED):
         g.wait_ge(T.sem["st%d" % k], n)
         send(k, "sin" if k < 3 else "sout")
-    g.wait_ge(T.sem.sout, 2 * sent)
+    g.wait_ge(T.sem.sout, 3 * sent)
 
     def level():
         wait(V, "cv", cnt["cv"])
@@ -279,12 +282,14 @@ def rank_program(g, core, T, topo):
             wait(P, "bd", 16)
             inc(P.matmul(T.p0a[:, 0:256], T.swp[:], T.hb[:], True, True), "hs")
         wait(P, "ev0", n)
-        wait(P, "v3", 4 * n)
-        P.matmul(T.pc[:, 0:256], T.upp[:], T.hot[:, 0:256], True, False)
+        wait(P, "w3", 2 * n)
         P.matmul(T.r0[:, 0:256], T.upp[:], T.hot[:, 256:512], True, False)
+        wait(P, "v3", 2 * n)
+        P.matmul(T.pc[:, 0:256], T.upp[:], T.hot[:, 0:256], True, False)
+        wait(P, "w4", n)
+        inc(P.matmul(T.r0[:, 0:256], T.one8[:], T.run[:, 256:512], False, True), "sc2")
         wait(P, "v4", n)
         inc(P.matmul(T.pc[:, 0:256], T.one8[:], T.run[:, 0:256], False, True), "sc")
-        inc(P.matmul(T.r0[:, 0:256], T.one8[:], T.run[:, 256:512], False, True), "sc2")
         if t == 0:
             wait(P, "ldx0", 16)
             wait(P, "ev1", 1)
@@ -293,11 +298,11 @@ def rank_program(g, core, T, topo):
             turn(5)
         wait(P, "v6", n)
         P.matmul(T.pa[:, 128:256], T.idf[:], T.blkf[:], True, False)
-        for sg in range(4):
+        for sg in (2, 3, 0, 1):
             if sg % 2 == 0:
                 wait(P, "v7" if sg == 0 else "s7", n)
             mm = P.matmul(T.pa[:, 128:256], T.coef[:, 128 * sg:128 * sg + 128], T.okk[:, 128 * sg:128 * sg + 128],
-                          False, sg == 3)
+                          False, sg == 1)
         inc(mm, "ss")
         if t == 0:
             wait(P, "shl", 1)
@@ -359,12 +364,14 @@ def rank_program(g, core, T, topo):
         inc(V.tensor_copy(T.ai[:], T.pa[:, 0:128]), "v1")
         wait(V, "v1", n)
         inc(ts(T.who[:], T.ai[:], N - 1, an), "v2")
-        wait(V, "v2", n)
-        for sg in range(4):
-            inc(ts(T.hot[:, 128 * sg:128 * sg + 128], T.who[:], T.slf[:, sg:sg + 1], A.is_equal), "v3")
-        wait(V, "v3", 4 * n)
-        inc(V.tensor_tensor_scan(T.run[:], T.keep[:], T.hot[:], 0.0, A.mult, A.add), "v4")
         inc(ts(T.blk[:], T.ai[:], 3, sr, WB - 1, an), "v5")
+        wait(V, "v2", n)
+        for sg in (2, 3, 0, 1):
+            inc(ts(T.hot[:, 128 * sg:128 * sg + 128], T.who[:], T.slf[:, sg:sg + 1], A.is_equal), "w3" if sg > 1 else "v3")
+        wait(V, "w3", 2 * n)
+        inc(V.tensor_tensor_scan(T.run[:, 256:512], T.keep[:, 256:512], T.hot[:, 256:512], 0.0, A.mult, A.add), "w4")
+        wait(V, "v3", 2 * n)
+        inc(V.tensor_tensor_scan(T.run[:, 0:256], T.keep[:, 0:256], T.hot[:, 0:256], 0.0, A.mult, A.add), "v4")
         wait(V, "v5", n)
         inc(V.tensor_copy(T.blkf[:], T.blk[:]), "v6")
         wait(V, "sc", n)
@@ -383,16 +390,17 @@ def rank_program(g, core, T, topo):
 
     for h in range(2):
         wait(Y, "n%d" % h, WAVES)
-        Y.dma_start(T.d1[:, 64 * h:64 * h + 64, :], W[:, cols(0, 1, h)]).then_inc(T.sem.st4, 16)
-    Y.wait_ge(T.sem.st4, 32)
-    own(4)
-    S.wait_ge(T.sem.sout, 2 * sent)
+        Y.dma_start(T[SRC[4 + h]][:], W[:, cols(0, 1, h)]).then_inc(T.sem["st%d" % (4 + h)], 16)
+    for h in range(2):
+        Y.wait_ge(T.sem["st%d" % (4 + h)], 16)
+        own(4 + h)
+    S.wait_ge(T.sem.sout, 3 * sent)
     S.wait_ge(T.sem.ar3, come)
     for h in range(2):
         S.dma_start(T.y[:, 512 * h:512 * h + 512], T.ya[:, 64 * h:64 * h + 64, :]).then_inc(T.sem.fin, 16)
-    for h, q in enumerate((Y, S)):
-        q.wait_ge(T.sem.ar4, come)
-        q.dma_start(T.y[:, SL + 512 * h:SL + 512 * h + 512], T.yb[:, 64 * h:64 * h + 64, :]).then_inc(T.sem.fin, 16)
+    for h in range(2):
+        Y.wait_ge(T.sem["ar%d" % (4 + h)], come)
+        Y.dma_start(T.y[:, SL + 512 * h:SL + 512 * h + 512], T[DST[4 + h]][:]).then_inc(T.sem.fin, 16)
     Y.wait_ge(T.sem.fin, 64)
     for name in cnt:
         if seen.get(name, 0) < cnt[name]:

@@ -4,23 +4,45 @@ from concourse.mybir import AluOpType as A, ActivationFunctionType as F
 N, SL, WB, CAP, WAVES = 8, 1024, 2048, 160, 4
 ZC = 4 * WB
 BIG = 2048
-COEF = [float(-ZC), float(WB - ZC), (2 * WB - ZC) / 2, (3 * WB - ZC) / 2]
+HALF = [(sg * WB - ZC) / 2 for sg in range(4)]
+PARTS = {"A": (0, 512), "B": (512, 768), "C": (768, 1024)}
+LISTS = {"A": (0, 64), "B": (64, 128)}
+KIND = [0, 1, 1, 2]
+CUTS = [[0, 32, 64, 96, 116, 128], [0, 30, 64, 86, 106, 128], [0, 24, 64, 104, 114, 128]]
+OUT = [["A"], ["B"], ["C"]]
+BY_DMA_A, BY_DMA_B = [1, 2], [2]
+FIRST_DMA = [(0, 0), (2, 1), (2, 0), (1, 0), (1, 1)]
+FIRST_PE = [(3, 1, 0), (3, 1, 1), (3, 0, 0), (3, 0, 1)]
+ORDER = [{
+    "V": "aiA whoA blkA hotA aiB scanA whoB blkfA hotB carry scanB blkB blkfB offA offB g1 g4 g2 nA nC nB".split(),
+    "S": "shl ev0 ev1 cmpA cmpB ev2 ev3 g0 g3 qA qC qB".split(),
+    "P": "hs namA namB pr0 pr1 upA cntA pr2 bkA upB finA cntB pr3 bkB finB baseA baseB baseC hA hC hB".split(),
+}, {
+    "V": "aiA whoA blkA hotA aiB scanA whoB blkfA hotB carry scanB blkB blkfB offA g1 offB g4 g2 nA nC nB".split(),
+    "S": "ev0 ev1 cmpA ev2 cmpB g0 g3 qA qC qB".split(),
+    "P": "namA pr0 namB pr1 pr2 upA cntA baseB bkA upB finA cntB baseA bkB finB hA baseC hC hB".split(),
+}, {
+    "V": "aiA whoA blkA hotA aiB scanA whoB blkfA hotB carry scanB blkB offA blkfB g1 offB g2 nA nB nC".split(),
+    "S": "ev0 ev1 cmpA ev2 cmpB g0 qA g3 g4 qB qC".split(),
+    "P": "namA pr0 namB pr1 pr2 upA cntA baseB bkA finA upB cntB baseA bkB finB hA baseC hB hC".split(),
+}]
 
 SCRATCH = {
-    "dp": ("dram", [8, 128, 64], "bfloat16"), "lp": ("dram", [8, 128, 64], "bfloat16"),
+    "dk": ("dram", [128, 1], "bfloat16"), "lk": ("dram", [8, 128, 1], "bfloat16"),
+    "dg": ("dram", [8, 128, 32], "bfloat16"), "lg": ("dram", [8, 128, 32], "bfloat16"),
     "d1": ("dram", [8, 128, 128], "bfloat16"), "l1": ("dram", [8, 128, 128], "bfloat16"),
     "d0": ("dram", [8, 128, 128], "bfloat16"), "l0": ("dram", [8, 128, 128], "bfloat16"),
-    "ya": ("dram", [8, 128, 128], "bfloat16"),
-    "db": ("dram", [8, 128, 64], "bfloat16"), "yb": ("dram", [8, 128, 64], "bfloat16"),
-    "yc": ("dram", [8, 128, 64], "bfloat16"),
+    "e0": ("dram", [8, 128, 128], "bfloat16"), "y0": ("dram", [8, 128, 128], "bfloat16"),
     "win": ("sbuf", [128, ZC + 16], "bfloat16"),
     "ref": ("sbuf", [128, 2048], "bfloat16"),
-    "tq": ("sbuf", [128, SL], "bfloat16"),
+    "tq": ("sbuf", [128, SL], "bfloat16"), "last": ("sbuf", [128, SL], "bfloat16"),
     "off": ("sbuf", [128, 128], "uint16"),
     "ai": ("sbuf", [128, 128], "int32"), "who": ("sbuf", [128, 128], "int32"), "blk": ("sbuf", [128, 128], "int32"),
     "blkf": ("sbuf", [128, 128], "float32"),
-    "hot": ("sbuf", [128, 512], "bfloat16"), "run": ("sbuf", [128, 512], "bfloat16"), "okk": ("sbuf", [128, 512], "bfloat16"),
-    "keep": ("sbuf", [128, 512], "bfloat16"), "ones": ("sbuf", [128, 512], "bfloat16"),
+    "hotA": ("sbuf", [128, 256], "bfloat16"), "runA": ("sbuf", [128, 256], "bfloat16"), "keepA": ("sbuf", [128, 256], "bfloat16"),
+    "hotB": ("sbuf", [128, 260], "bfloat16"), "runB": ("sbuf", [128, 260], "bfloat16"), "keepB": ("sbuf", [128, 260], "bfloat16"),
+    "okA": ("sbuf", [128, 256], "bfloat16"), "okB": ("sbuf", [128, 256], "bfloat16"),
+    "ones": ("sbuf", [128, 512], "bfloat16"),
     "jj": ("sbuf", [128, 128], "int32"), "pp": ("sbuf", [128, 8], "int32"),
     "ti": ("sbuf", [128, 384], "int32"), "tk": ("sbuf", [128, 256], "float32"),
     "ci": ("sbuf", [128, 16], "int32"), "cf": ("sbuf", [128, 16], "float32"), "cg": ("sbuf", [128, 8], "float32"),
@@ -31,19 +53,23 @@ SCRATCH = {
     "msk": ("sbuf", [128, 1024], "bfloat16"), "lw": ("sbuf", [128, 1024], "bfloat16"), "c258": ("sbuf", [128, 128], "bfloat16"),
     "wc": ("sbuf", [128, 16], "bfloat16"), "gcb": ("sbuf", [128, 16], "bfloat16"), "hc": ("sbuf", [128, 16], "bfloat16"),
     "gbd": ("sbuf", [128, 128], "bfloat16"), "hb": ("sbuf", [128, 256], "bfloat16"), "hl": ("sbuf", [128, 256], "bfloat16"),
-    "p0a": ("psum", [128, 512], "float32"), "p0b": ("psum", [128, 512], "float32"),
-    "p1a": ("psum", [128, 512], "float32"), "p1b": ("psum", [128, 512], "float32"),
-    "pa": ("psum", [128, 512], "float32"), "pc": ("psum", [128, 512], "float32"),
+    "vA": ("psum", [128, 512], "float32"), "vB": ("psum", [128, 512], "float32"), "vC": ("psum", [128, 512], "float32"),
+    "bA": ("psum", [128, 512], "float32"), "bB": ("psum", [128, 512], "float32"), "pf": ("psum", [128, 512], "float32"),
     "r0": ("psum", [128, 512], "float32"), "r1": ("psum", [128, 512], "float32"),
 }
-SEMAPHORES = (["iot", "cv", "sin", "sout",
-               "ldw", "ldg", "ldx1", "ldx0", "repd", "slw", "bd", "hs", "shl", "sa", "v1", "v2", "v3", "w3", "v4", "w4", "v5",
-               "v6", "sc", "sc2", "v7", "s7", "ss", "v8", "ph0", "ph1", "q0", "q1", "n0", "n1", "fin"]
-              + ["st%d" % i for i in range(6)] + ["ar%d" % i for i in range(6)]
-              + ["ga%d" % i for i in range(4)] + ["pr%d" % i for i in range(6)] + ["ev%d" % i for i in range(6)])
-SRC = ["dp", "d1", "d0", "d0", "dp", "db"]
-DST = ["lp", "l1", "l0", "ya", "yb", "yc"]
-STAGED = [80, 16, 16, 32, 16, 16]
+SRC = ["dk", "dg", "d1", "d0", "e0"]
+DST = ["lk", "lg", "l1", "l0", "y0"]
+STAGED = [16, 32, 16, 16, 16]
+for x, ps in enumerate(OUT):
+    width = (PARTS[ps[-1]][1] - PARTS[ps[0]][0]) // 8
+    SCRATCH["e%d" % (x + 1)] = ("dram", [8, 128, width], "bfloat16")
+    SCRATCH["y%d" % (x + 1)] = ("dram", [8, 128, width], "bfloat16")
+    SRC.append("e%d" % (x + 1))
+    DST.append("y%d" % (x + 1))
+    STAGED.append(16)
+SEMAPHORES = (["iot", "cv", "snt", "ldw", "ldg", "ldx1", "ldx0", "rep", "slw", "bdv", "bds", "fin"]
+              + sorted(set(sum(ORDER[0].values(), []) + ["ev4", "ev5", "pr4", "pr5"]))
+              + ["st%d" % i for i in range(len(SRC))] + ["ar%d" % i for i in range(len(SRC))])
 
 
 def bits(engines):
@@ -74,8 +100,8 @@ def helper_program(g, core, T, topo):
             eng = topo.engines(core, dst)[0::2]
             for k in range(len(DST)):
                 g.wait_ge(T.sem["ar%d" % k], 2)
-                g.remote_dma(T[DST[k]][r], T[DST[k]][0], T.sem["ar%d" % k], T.sem.sin, pid, rid, bits(eng))
-            g.wait_ge(T.sem.sin, len(DST) * len(eng))
+                g.remote_dma(T[DST[k]][r], T[DST[k]][0], T.sem["ar%d" % k], T.sem.snt, pid, rid, bits(eng))
+            g.wait_ge(T.sem.snt, len(DST) * len(eng))
 
 
 def rank_program(g, core, T, topo):
@@ -104,41 +130,42 @@ def rank_program(g, core, T, topo):
     sent = len(near) + 2 * len(far)
     come = 16 + len(near) + len(far) * len(off_eng[0::2])
 
-    def send(k, lsem):
+    def piece(k, q):
+        return T.dk[:] if k == 0 else T[SRC[k]][q]
+
+    def send(k):
         out = []
         for h, q in far:
             rid, pid = topo.addr(h, core)
             out.append(RemoteDMATransfer(dst_ids=[DstId(rid=rid, pnc=pid)], dma_engine_mask=hmask[h],
-                                         remote_sem=T.sem["ar%d" % k], src=T[SRC[k]][q], dst=T[DST[k]][0]))
+                                         remote_sem=T.sem["ar%d" % k], src=piece(k, q), dst=T[DST[k]][0]))
         for x, q in enumerate(near):
             rid, pid = topo.addr(T.cores[q], core)
             out.append(RemoteDMATransfer(dst_ids=[DstId(rid=rid, pnc=pid)], dma_engine_mask=bits([off_eng[2 * x]]),
-                                         remote_sem=T.sem["ar%d" % k], src=T[SRC[k]][q], dst=T[DST[k]][me]))
-        g.remote_dma_fused(out, local_sem=T.sem[lsem])
+                                         remote_sem=T.sem["ar%d" % k], src=piece(k, q), dst=T[DST[k]][me]))
+        g.remote_dma_fused(out, local_sem=T.sem.snt)
 
-    def own(k):
-        Y.dma_start(T[DST[k]][me], T[SRC[k]][me]).then_inc(T.sem["ar%d" % k], 16)
+    def own(k, q=Y):
+        q.wait_ge(T.sem["st%d" % k], STAGED[k])
+        q.dma_start(T[DST[k]][me], piece(k, me)).then_inc(T.sem["ar%d" % k], 16)
 
     W = T.win
 
-    def cols(sg, s, h=None):
-        a = sg * WB + s * SL
-        return slice(a, a + SL) if h is None else slice(a + 512 * h, a + 512 * h + 512)
+    def cols(sg, s, a=0, b=SL):
+        return slice(sg * WB + s * SL + a, sg * WB + s * SL + b)
 
-    Y.dma_start(T.dp[:, 64, 0:16], T.kw[:]).then_inc(T.sem.st0, 16)
-    Y.dma_start(T.dp[:, 64, 16:64], T.m[:, 0:3]).then_inc(T.sem.st0, 16)
-    Y.dma_start(T.dp[:, 65:128, :], T.m[:, 0:252]).then_inc(T.sem.st0, 16)
-    S.dma_start(T.dp[:, 0:32, :], T.gm[:]).then_inc(T.sem.st0, 16)
-    S.dma_start(T.dp[:, 32:64, :], T.hm[:]).then_inc(T.sem.st0, 16)
-    S.dma_start(T.d1[:], T.m[:, SL:WB]).then_inc(T.sem.st1, 16)
-    Y.dma_start(T.d0[:], T.m[:, 0:SL]).then_inc(T.sem.st2, 16)
+    Y.dma_start(T.dk[:], T.kw[:]).then_inc(T.sem.st0, 16)
+    S.dma_start(T.dg[:, 0:64, :], T.gm[:]).then_inc(T.sem.st1, 16)
+    Y.dma_start(T.dg[:, 64:128, :], T.hm[:]).then_inc(T.sem.st1, 16)
+    S.dma_start(T.d1[:], T.m[:, SL:WB]).then_inc(T.sem.st2, 16)
+    Y.dma_start(T.d0[:], T.m[:, 0:SL]).then_inc(T.sem.st3, 16)
 
     inc(g.iota(T.jj[:], [[1, 128]], 0, 0), "iot")
     inc(g.iota(T.pp[:], [[0, 8]], 0, 1), "iot")
     for k, n in enumerate(STAGED):
         g.wait_ge(T.sem["st%d" % k], n)
-        send(k, "sin" if k < 3 else "sout")
-    g.wait_ge(T.sem.sout, 3 * sent)
+        send(k)
+    g.wait_ge(T.sem.snt, len(SRC) * sent)
 
     def level():
         wait(V, "cv", cnt["cv"])
@@ -149,23 +176,24 @@ def rank_program(g, core, T, topo):
         return V.tensor_scalar(out, in0, s1, s2, op0, op1)
 
     inc(V.memset(T.ones[:], 1.0), "cv")
-    inc(V.memset(T.keep[:], 1.0), "cv")
+    inc(V.memset(T.keepA[:], 1.0), "cv")
+    inc(V.memset(T.keepB[:], 1.0), "cv")
     inc(V.memset(T.c258[:], 258.0), "cv")
     inc(V.memset(T.hb[:], 0.0), "cv")
     inc(V.memset(W[:, ZC:ZC + 16], 0.0), "cv")
     wait(V, "iot", 2)
     sr, an = A.logical_shift_right, A.bitwise_and
     J, pc0 = T.jj, T.pp[:, 0:1]
-    inc(ts(T.ti[:, 0:128], J[:], 3, sr), "cv")
+    inc(ts(T.ti[:, 0:128], J[:], 0x71, an), "cv")
     inc(ts(T.ti[:, 128:256], J[:], 5, sr), "cv")
     inc(ts(T.ti[:, 256:384], J[:], 15, an), "cv")
     inc(V.tensor_copy(T.ci[:, 0:1], pc0), "cv")
-    inc(ts(T.ci[:, 1:2], pc0, 3, sr), "cv")
+    inc(ts(T.ci[:, 1:2], pc0, 0x71, an), "cv")
     inc(ts(T.ci[:, 2:3], pc0, 4, sr), "cv")
     inc(ts(T.ci[:, 3:4], pc0, 5, sr), "cv")
     inc(ts(T.ci[:, 4:5], pc0, 15, an), "cv")
     inc(ts(T.ci[:, 5:6], pc0, 4, sr, 1, an), "cv")
-    inc(ts(T.ci[:, 6:7], pc0, 3, sr, 1, an), "cv")
+    inc(ts(T.ci[:, 6:7], pc0, 1, an), "cv")
     level()
     inc(V.tensor_copy(T.cf[:, 0:7], T.ci[:, 0:7]), "cv")
     inc(ts(T.tk[:, 0:128], T.ti[:, 128:256], 16.0, A.mult), "cv")
@@ -173,7 +201,7 @@ def rank_program(g, core, T, topo):
     cf = T.cf
     inc(V.tensor_tensor(T.tk[:, 128:256], T.tk[:, 0:128], T.ti[:, 256:384], A.add), "cv")
     inc(ts(T.cg[:, 0:1], cf[:, 3:4], 16.0, A.mult, cf[:, 4:5], A.add), "cv")
-    inc(ts(T.cg[:, 1:2], cf[:, 3:4], 2.0, A.mult, cf[:, 5:6], A.add), "cv")
+    inc(ts(T.cg[:, 2:3], cf[:, 3:4], 16.0, A.mult, cf[:, 5:6], A.add), "cv")
     inc(V.tensor_tensor(T.cg[:, 3:4], cf[:, 5:6], cf[:, 6:7], A.not_equal), "cv")
     inc(ts(T.sli[:, 0:4], J[:, 0:4], 2.0, A.mult, cf[:, 2:3], A.add), "cv")
     inc(ts(T.grp[:], J[:, 0:8], cf[:, 2:3], A.is_equal), "cv")
@@ -181,227 +209,220 @@ def rank_program(g, core, T, topo):
     inc(ts(T.id2[:, 128:256], J[:], cf[:, 0:1], A.is_equal), "cv")
     inc(ts(T.idf[:], J[:], cf[:, 0:1], A.is_equal), "cv")
     for sg in range(4):
-        inc(ts(T.coef[:, 128 * sg:128 * sg + 128], J[:], cf[:, 0:1], A.is_equal, COEF[sg], A.mult), "cv")
+        inc(ts(T.coef[:, 128 * sg:128 * sg + 128], J[:], cf[:, 0:1], A.is_equal, HALF[sg], A.mult), "cv")
     inc(ts(T.one8[:], T.ti[:, 0:128], cf[:, 1:2], A.is_equal), "cv")
     inc(ts(T.low[:, 0:128], J[:], cf[:, 0:1], A.is_lt, -1.0, A.mult), "cv")
     level()
-    inc(ts(T.cg[:, 2:3], T.cg[:, 1:2], 8.0, A.mult), "cv")
     inc(ts(T.sli[:, 4:8], T.sli[:, 0:4], 7, an), "cv")
     inc(V.tensor_tensor(T.low[:, 128:256], T.low[:, 0:128], T.one8[:], A.mult), "cv")
     inc(ts(T.swp[:], T.tk[:, 128:256], T.cg[:, 0:1], A.is_equal), "cv")
-    inc(ts(T.keep[:, 0:128], T.ones[:, 0:128], T.cg[:, 3:4], A.mult), "cv")
+    inc(ts(T.keepA[:, 0:64], T.ones[:, 0:64], T.cg[:, 3:4], A.mult), "cv")
+    inc(ts(T.keepB[:, 0:65], T.ones[:, 0:65], T.cg[:, 3:4], A.mult), "cv")
     level()
     inc(V.tensor_copy(T.slf[:], T.sli[:, 4:8]), "cv")
     inc(V.tensor_tensor(T.upp[:], T.low[:, 128:256], T.coef[:, 256:384], A.add), "cv")
-    inc(V.memset(T.keep[:, 0:512:128], 0.0), "cv")
+    inc(V.memset(T.keepA[:, 0:256:64], 0.0), "cv")
+    inc(V.memset(T.keepB[:, 0:260:65], 0.0), "cv")
     for e in range(8):
-        inc(ts(T.msk[:, 128 * e:128 * e + 128], T.tk[:, 128:256], float(e), A.subtract, T.cg[:, 2:3], A.is_equal), "cv")
+        inc(ts(T.msk[:, 128 * e:128 * e + 128], T.tk[:, 128:256], 2.0 * e, A.subtract, T.cg[:, 2:3], A.is_equal), "cv")
     level()
     consts = cnt["cv"]
     wait(V, "ldw", 16)
     inc(ts(T.lw[:], T.msk[:], T.wc[:, 0:1], A.mult), "slw")
 
-    for k in range(3):
-        Y.wait_ge(T.sem["st%d" % k], STAGED[k])
+    for k in range(4):
         own(k)
-
-    def turned(sg, s, src):
-        inc(Y.dma_start(W[0:128 - 32 * sg, cols(sg, s)], src[2 * sg:8]), "repd", 16)
-        inc(Y.dma_start(W[128 - 32 * sg:128, cols(sg, s)], src[0:2 * sg]), "repd", 16)
-
-    Y.wait_ge(T.sem.ar0, come)
-    inc(Y.dma_start(T.wc[:, 0:1], T.lp[:, 64, 0:16]), "ldw", 16)
-    Y.wait_ge(T.sem.ar1, come)
-    inc(Y.dma_start(W[:, cols(0, 1)], T.l1[:]), "ldx1", 16)
-    turned(2, 1, T.l1)
-    Y.wait_ge(T.sem.ar2, come)
-    inc(Y.dma_start(W[:, cols(0, 0)], T.l0[:]), "ldx0", 16)
-    turned(2, 0, T.l0)
-    turned(1, 0, T.l0)
-
     S.wait_ge(T.sem.ar0, come)
-    row, c0 = me // 4, (16 * me) % 64
-    inc(S.dma_start(T.gcb[:], T.lp[:, row:32:2, c0:c0 + 16]), "ldg", 16)
-    inc(S.dma_start(T.hc[:], T.lp[:, 32 + row:64:2, c0:c0 + 16]), "ldg", 16)
+    inc(S.dma_start(T.wc[:, 0:1], T.lk[:, 16 * me:16 * me + 16, 0]), "ldw", 16)
+    S.wait_ge(T.sem.ar1, come)
+    row, c0 = me // 2, (16 * me) % 32
+    inc(S.dma_start(T.hc[:], T.lg[:, 64 + row:128:4, c0:c0 + 16]), "ldg", 16)
+    inc(S.dma_start(T.gcb[:], T.lg[:, row:64:4, c0:c0 + 16]), "ldg", 16)
     wait(S, "cv", consts)
     wait(S, "ldg", 32)
     for r in range(8):
         a = 128 * (r % 2) + 16 * r
-        inc(S.activation(T.hb[:, a:a + 16], T.hc[:], F.Copy, scale=T.grp[:, r:r + 1]), "bd")
+        inc(S.activation(T.hb[:, a:a + 16], T.hc[:], F.Copy, scale=T.grp[:, r:r + 1]), "bds")
+    wait(V, "ldg", 32)
     for r in range(8):
-        inc(S.activation(T.gbd[:, 16 * r:16 * r + 16], T.gcb[:], F.Copy, scale=T.grp[:, r:r + 1]), "bd")
+        inc(ts(T.gbd[:, 16 * r:16 * r + 16], T.gcb[:], T.grp[:, r:r + 1], A.mult), "bdv")
     wait(P, "cv", consts)
 
-    banks = [[T.p0a, T.p0b], [T.p1a, T.p1b]]
-    ident = T.id2[:, 0:128]
+    def turned(sg, dst, src):
+        inc(Y.dma_start(W[0:128 - 32 * sg, dst], src(32 * sg, 128)), "rep", 16)
+        inc(Y.dma_start(W[128 - 32 * sg:128, dst], src(0, 32 * sg)), "rep", 16)
 
-    def base(t, b):
-        P.matmul(banks[t % 2][b][:], T.c258[:], T.ones[:], True, False)
-        P.matmul(banks[t % 2][b][:], ident, W[:, cols(0, t % 2, b)], False, False)
-
-    for t in range(WAVES):
-        s, sp, n = t % 2, (t + 1) % 2, t + 1
-        mine, other = banks[t % 2], banks[(t + 1) % 2]
-        jobs = [(1, sp, 0, T.r0), (3, sp, 0, other[0]), (1, sp, 1, T.r1), (3, sp, 1, other[1])]
-        if t == 0:
-            jobs += [(3, 0, 0, other[0]), (3, 0, 1, T.r1)]
-
-        def turn(x):
-            sg, sl, h, bank = jobs[x]
-            inc(P.matmul(bank[:], T.id2[:, 32 * sg:32 * sg + 128], W[:, cols(0, sl, h)], True, True), "pr%d" % x)
-
-        def evac(x):
-            sg, sl, h, bank = jobs[x]
-            wait(S, "pr%d" % x, n)
-            inc(S.activation(W[:, cols(sg, sl, h)], bank[:], F.Copy), "ev%d" % x)
-
-        def gprev(b):
-            P.matmul(mine[b][:], T.gbd[:], W[:, cols(0, sp, b)], False, False)
-
-        def named(k0, k1):
-            for e in range(8):
-                a = sp * SL
-                mm = P.matmul(T.pa[:, k0:k1], T.lw[:, 128 * e:128 * e + 128], W[:, a + 8 * k0 + e:a + 8 * k1:8], e == 0, e == 7)
-            inc(mm, "sa")
-
-        if t == 0:
-            wait(P, "slw", 1)
-            wait(P, "ldx1", 16)
-            named(0, 128)
-            turn(0)
+    land = [T.l0, T.l1]
+    Y.wait_ge(T.sem.ar2, come)
+    inc(Y.dma_start(W[:, cols(0, 1)], T.l1[:]), "ldx1", 16)
+    here = [False, True]
+    for sg, s in FIRST_DMA:
+        if not here[s]:
+            Y.wait_ge(T.sem.ar3, come)
+            here[s] = True
+        if sg == 0:
+            inc(Y.dma_start(W[:, cols(0, s)], land[s][:]), "ldx0", 16)
         else:
-            wait(P, "n0", t)
-            named(0, 64)
-            turn(0)
-            wait(P, "n1", t)
-            named(64, 128)
-        turn(1)
-        turn(2)
-        turn(3)
-        if t == 0:
-            wait(P, "bd", 16)
-            inc(P.matmul(T.p0a[:, 0:256], T.swp[:], T.hb[:], True, True), "hs")
-        wait(P, "ev0", n)
-        wait(P, "w3", 2 * n)
-        P.matmul(T.r0[:, 0:256], T.upp[:], T.hot[:, 256:512], True, False)
-        wait(P, "v3", 2 * n)
-        P.matmul(T.pc[:, 0:256], T.upp[:], T.hot[:, 0:256], True, False)
-        wait(P, "w4", n)
-        inc(P.matmul(T.r0[:, 0:256], T.one8[:], T.run[:, 256:512], False, True), "sc2")
-        wait(P, "v4", n)
-        inc(P.matmul(T.pc[:, 0:256], T.one8[:], T.run[:, 0:256], False, True), "sc")
-        if t == 0:
-            wait(P, "ldx0", 16)
-            wait(P, "ev1", 1)
-            turn(4)
-            wait(P, "ev2", 1)
-            turn(5)
-        wait(P, "v6", n)
-        P.matmul(T.pa[:, 128:256], T.idf[:], T.blkf[:], True, False)
-        for sg in (2, 3, 0, 1):
-            if sg % 2 == 0:
-                wait(P, "v7" if sg == 0 else "s7", n)
-            mm = P.matmul(T.pa[:, 128:256], T.coef[:, 128 * sg:128 * sg + 128], T.okk[:, 128 * sg:128 * sg + 128],
-                          False, sg == 1)
-        inc(mm, "ss")
-        if t == 0:
-            wait(P, "shl", 1)
-            base(0, 0)
-        gprev(0)
-        if t == 0:
-            base(0, 1)
-        gprev(1)
-        for b in range(2):
-            wait(P, "ga%d" % (2 * b), n)
-            wait(P, "ga%d" % (2 * b + 1), n)
-            for c in range(16):
-                q, e = c // 8, c % 8
-                mm = P.matmul(mine[b][:, e:512:8], T.hl[:, 128 * q:128 * q + 128], T.ref[:, SL * b + c:SL * b + SL:16],
-                              False, c == 15)
-            inc(mm, "ph%d" % b)
-        if t + 1 < WAVES:
-            base(t + 1, 0)
-            base(t + 1, 1)
+            turned(sg, cols(sg, s), lambda a, b: land[s][a // 16:b // 16])
 
+    ident = T.id2[:, 0:128]
+    queue = {"V": V, "S": S, "P": P}
+    total = {}
+
+    def order(q, t):
+        return ORDER[KIND[t]][q]
+
+    def copy(name, t, out, src):
+        return [V.tensor_copy(out, src) if name in order("V", t) else S.activation(out, src, F.Copy)]
+
+    def steps(t):
+        s, sp = t % 2, (t + 1) % 2
+        st = {}
+        cut = CUTS[KIND[t]]
+        gathers = {"g%d" % x: (cut[x], cut[x + 1]) for x in range(len(cut) - 1)}
+
+        def made(parts):
+            return [("n" + x, t - 1) for x in parts] if t else [("ldx1", None)]
+
+        def into(x):
+            a, b = PARTS[x]
+            return T.last[:, a:b] if t + 1 == WAVES else W[:, cols(0, s, a, b)]
+
+        if t == 0:
+            jobs = [(sg, sl, h, [("ldx%d" % sl, None)]) for sg, sl, h in FIRST_PE]
+            st["hs"] = ([("bds", None)], 1, lambda: [P.matmul(T.pf[:, 0:256], T.swp[:], T.hb[:], True, True)])
+            st["shl"] = ([("hs", 0)], 1, lambda: [S.activation(T.hl[:], T.pf[:, 0:256], F.Copy)])
+        else:
+            jobs = ([(sg, sp, 0, made("A")) for sg in (1, 2, 3) if sg not in BY_DMA_A]
+                    + [(sg, sp, 1, made("BC")) for sg in (1, 2, 3) if sg not in BY_DMA_B])
+        for x, (sg, sl, h, dep) in enumerate(jobs):
+            bank = [T.r0, T.r1][x % 2]
+            st["pr%d" % x] = (dep + ([("ev%d" % (x - 2), t)] if x > 1 else []), 1, lambda sg=sg, sl=sl, h=h, bank=bank: [
+                P.matmul(bank[:], T.id2[:, 32 * sg:32 * sg + 128], W[:, cols(0, sl, 512 * h, 512 * h + 512)], True, True)])
+            st["ev%d" % x] = ([("pr%d" % x, t)], 1, lambda x=x, sg=sg, sl=sl, h=h, bank=bank: copy(
+                "ev%d" % x, t, W[:, cols(sg, sl, 512 * h, 512 * h + 512)], bank[:]))
+        window = [("rep", None)] + [("ev%d" % x, t) for x in range(len(jobs))]
+
+        for x, (k0, k1) in LISTS.items():
+            k, bank, lead = slice(k0, k1), T["b" + x], int(x == "B")
+            hot, run, ok, w = T["hot" + x], T["run" + x], T["ok" + x], 64 + lead
+
+            def named(k0=k0, k1=k1, bank=bank):
+                for e in range(8):
+                    a = sp * SL
+                    mm = P.matmul(bank[:, 0:64], T.lw[:, 128 * e:128 * e + 128], W[:, a + 8 * k0 + e:a + 8 * k1:8], e == 0, e == 7)
+                return [mm]
+
+            def count(lhs, src, first, bank=bank, lead=lead, w=w):
+                if lead:
+                    for sg in range(4):
+                        mm = P.matmul(bank[:, 64 + 64 * sg:128 + 64 * sg], lhs, src[:, w * sg + 1:w * sg + w],
+                                      first and sg == 0, not first and sg == 3)
+                else:
+                    mm = P.matmul(bank[:, 64:320], lhs, src[:], first, not first)
+                return [] if first else [mm]
+
+            def block(k=k):
+                P.matmul(T.pf[:, k], T.idf[:], T.blkf[:, k], True, False)
+                return []
+
+            def final(k=k, ok=ok):
+                for sg in range(4):
+                    mm = P.matmul(T.pf[:, k], T.coef[:, 128 * sg:128 * sg + 128], ok[:, 64 * sg:64 * sg + 64], False, sg == 3)
+                return [mm]
+
+            on_s = "cmp" + x in order("S", t)
+            st["nam" + x] = (made("A" if x == "A" else "BC") + ([("slw", None)] if t == 0 else []), 1, named)
+            st["ai" + x] = ([("nam" + x, t)], 1, lambda k=k, bank=bank: [V.tensor_copy(T.ai[:, k], bank[:, 0:64])])
+            st["who" + x] = ([("ai" + x, t)], 1, lambda k=k: [ts(T.who[:, k], T.ai[:, k], N - 1, an)])
+            st["blk" + x] = ([("ai" + x, t)], 1, lambda k=k: [ts(T.blk[:, k], T.ai[:, k], 3, sr, WB - 1, an)])
+            st["blkf" + x] = ([("blk" + x, t)], 1, lambda k=k: [V.tensor_copy(T.blkf[:, k], T.blk[:, k])])
+            st["hot" + x] = ([("who" + x, t)], 4, lambda k=k, hot=hot, lead=lead, w=w: [
+                ts(hot[:, w * sg + lead:w * sg + w], T.who[:, k], T.slf[:, sg:sg + 1], A.is_equal) for sg in range(4)])
+            st["scan" + x] = ([("hot" + x, t)] + [("carry", t)] * lead, 1, lambda x=x, hot=hot, run=run: [
+                V.tensor_tensor_scan(run[:], T["keep" + x][:], hot[:], 0.0, A.mult, A.add)])
+            st["up" + x] = ([("hot" + x, t)] + [("carry", t)] * lead, 0, lambda count=count, hot=hot: count(T.upp[:], hot, True))
+            st["cnt" + x] = ([("scan" + x, t)], 1, lambda count=count, run=run: count(T.one8[:], run, False))
+            st["cmp" + x] = ([("cnt" + x, t)], 1, lambda bank=bank, ok=ok, on_s=on_s: [
+                S.activation(ok[:], bank[:, 64:320], F.Sign, bias=CAP - BIG + 0.5, scale=-1.0) if on_s else
+                ts(ok[:], bank[:, 64:320], float(CAP - BIG), A.is_le, 2.0, A.mult)])
+            st["bk" + x] = ([("blkf" + x, t)] + ([("offA", t)] if lead else [("shl", 0)] * (t == 0)), 0, block)
+            st["fin" + x] = ([("cmp" + x, t)], 1, final)
+            st["off" + x] = ([("fin" + x, t)], 1, lambda k=k, on_s=on_s: [
+                ts(T.off[:, k], T.pf[:, k], ZC + sum(HALF) * on_s, A.add, float(ZC), A.min)])
+        st["carry"] = ([("scanA", t)], 1, lambda: copy("carry", t, T.hotB[:, 0:260:65], T.runA[:, 63:256:64]))
+
+        for x, (k0, k1) in gathers.items():
+            st[x] = (window + [("offA", t)] * (k0 < 64) + [("offB", t)] * (k1 > 64), 1, lambda x=x, k0=k0, k1=k1: copy(
+                x, t, T.ref[:, 16 * k0:16 * k1], W[:, 0:ZC + 16].indirect(T.off[:, k0:k1])))
+
+        for x, (a, b) in PARTS.items():
+            bank, n = T["v" + x], b - a
+
+            def base(a=a, b=b, bank=bank, n=n):
+                P.matmul(bank[:, 0:n], T.c258[:], T.ones[:, 0:n], True, False)
+                P.matmul(bank[:, 0:n], ident, W[:, cols(0, s, a, b)], False, False)
+                P.matmul(bank[:, 0:n], T.gbd[:], W[:, cols(0, sp, a, b)], False, False)
+                return []
+
+            def href(a=a, b=b, bank=bank, n=n):
+                for q in range(2):
+                    mm = P.matmul(bank[:, 0:n], T.hl[:, 128 * q:128 * q + 128], T.ref[:, 2 * a + q:2 * b:2], False, q == 1)
+                return [mm]
+
+            def quot(x=x, a=a, b=b, bank=bank, n=n):
+                if "q" + x in order("V", t):
+                    return [ts(T.tq[:, a:b], bank[:, 0:n], -127.5, A.add)]
+                return [S.activation(T.tq[:, a:b], bank[:, 0:n], F.Identity, bias=-127.5)]
+
+            st["base" + x] = (made(x) + ([("ldx0", None), ("bdv", None)] if t == 0 else []), 0, base)
+            st["h" + x] = ([(y, t) for y, (k0, k1) in gathers.items() if 8 * k0 < b and 8 * k1 > a], 1, href)
+            st["q" + x] = ([("h" + x, t)], 1, quot)
+            st["n" + x] = ([("q" + x, t)] + [(y, t) for y in gathers if t + 1 < WAVES], 1, lambda x=x, a=a, b=b, bank=bank, n=n: [
+                V.tensor_tensor(into(x), bank[:, 0:n], T.tq[:, a:b], A.subtract)])
+        return st
+
+    passed = {q: {} for q in queue}
+    for t in range(WAVES):
+        st, sp = steps(t), (t + 1) % 2
+        for name, (dep, n, calls) in st.items():
+            total[name, t] = cnt.get(name, 0) + n
         if t > 0:
-            for h in range(2):
-                wait(Y, "n%d" % h, t)
-                inc(Y.dma_start(W[0:64, cols(2, sp, h)], W[64:128, cols(0, sp, h)]), "repd", 16)
-                inc(Y.dma_start(W[64:128, cols(2, sp, h)], W[0:64, cols(0, sp, h)]), "repd", 16)
-        reps = cnt["repd"]
-        if t == 3:
-            Y.wait_ge(T.sem.sin, 3 * sent)
-            for h in range(2):
-                Y.dma_start(T.d0[:, 64 * h:64 * h + 64, :], W[:, cols(0, 0, h)]).then_inc(T.sem.st3, 16)
-            Y.wait_ge(T.sem.st3, 32)
-            own(3)
+            for parts, h, slots in (("A", 0, BY_DMA_A), ("BC", 1, BY_DMA_B)):
+                for x in parts:
+                    wait(Y, "n" + x, total["n" + x, t - 1])
+                for sg in slots:
+                    turned(sg, cols(sg, sp, 512 * h, 512 * h + 512), lambda a, b: W[a:b, cols(0, sp, 512 * h, 512 * h + 512)])
+        if t + 1 == WAVES:
+            Y.dma_start(T.e0[:], W[:, cols(0, 0)]).then_inc(T.sem.st4, 16)
+            own(4)
+        for q in queue:
+            for name in order(q, t):
+                if name not in st:
+                    continue
+                dep, n, calls = st[name]
+                for d, u in dep:
+                    need = cnt[d] if u is None else total[d, u]
+                    if passed[q].get(d, 0) < need:
+                        wait(queue[q], d, need)
+                        passed[q][d] = need
+                for ins in calls():
+                    inc(ins, name)
 
-        for x in range(4):
-            evac(x)
-        wait(S, "sc2", n)
-        inc(S.activation(T.okk[:, 256:512], T.r0[:, 0:256], F.Sign, bias=CAP - BIG + 0.5, scale=-1.0), "s7")
-        if t == 0:
-            wait(S, "hs", 1)
-            inc(S.activation(T.hl[:], T.p0a[:, 0:256], F.Copy), "shl")
-            evac(4)
-            evac(5)
-
-        def ready(q):
-            wait(q, "repd", reps)
-            for x in range(len(jobs)):
-                wait(q, "ev%d" % x, n)
-            wait(q, "v8", n)
-
-        ready(S)
-        for c in (1, 3):
-            inc(S.activation(T.ref[:, 512 * c:512 * c + 512], W[:, 0:ZC + 16].indirect(T.off[:, 32 * c:32 * c + 32]), F.Copy),
-                "ga%d" % c)
-        for b in range(2):
-            wait(S, "ph%d" % b, n)
-            inc(S.activation(T.tq[:, 512 * b:512 * b + 512], mine[b][:], F.Identity, bias=-127.5), "q%d" % b)
-
-        wait(V, "sa", cnt["sa"])
-        inc(V.tensor_copy(T.ai[:], T.pa[:, 0:128]), "v1")
-        wait(V, "v1", n)
-        inc(ts(T.who[:], T.ai[:], N - 1, an), "v2")
-        inc(ts(T.blk[:], T.ai[:], 3, sr, WB - 1, an), "v5")
-        wait(V, "v2", n)
-        for sg in (2, 3, 0, 1):
-            inc(ts(T.hot[:, 128 * sg:128 * sg + 128], T.who[:], T.slf[:, sg:sg + 1], A.is_equal), "w3" if sg > 1 else "v3")
-        wait(V, "w3", 2 * n)
-        inc(V.tensor_tensor_scan(T.run[:, 256:512], T.keep[:, 256:512], T.hot[:, 256:512], 0.0, A.mult, A.add), "w4")
-        wait(V, "v3", 2 * n)
-        inc(V.tensor_tensor_scan(T.run[:, 0:256], T.keep[:, 0:256], T.hot[:, 0:256], 0.0, A.mult, A.add), "v4")
-        wait(V, "v5", n)
-        inc(V.tensor_copy(T.blkf[:], T.blk[:]), "v6")
-        wait(V, "sc", n)
-        inc(ts(T.okk[:, 0:256], T.pc[:, 0:256], float(CAP - BIG), A.is_le), "v7")
-        wait(V, "ss", n)
-        inc(ts(T.off[:], T.pa[:, 128:256], ZC + COEF[2] + COEF[3], A.add, float(ZC), A.min), "v8")
-        ready(V)
-        for c in (0, 2):
-            inc(V.tensor_copy(T.ref[:, 512 * c:512 * c + 512], W[:, 0:ZC + 16].indirect(T.off[:, 32 * c:32 * c + 32])),
-                "ga%d" % c)
-        for c in range(4):
-            wait(V, "ga%d" % c, n)
-        for b in range(2):
-            wait(V, "q%d" % b, n)
-            inc(V.tensor_tensor(W[:, cols(0, s, b)], mine[b][:], T.tq[:, 512 * b:512 * b + 512], A.subtract), "n%d" % b)
-
-    for h in range(2):
-        wait(Y, "n%d" % h, WAVES)
-        Y.dma_start(T[SRC[4 + h]][:], W[:, cols(0, 1, h)]).then_inc(T.sem["st%d" % (4 + h)], 16)
-    for h in range(2):
-        Y.wait_ge(T.sem["st%d" % (4 + h)], 16)
-        own(4 + h)
-    S.wait_ge(T.sem.sout, 3 * sent)
-    S.wait_ge(T.sem.ar3, come)
-    for h in range(2):
-        S.dma_start(T.y[:, 512 * h:512 * h + 512], T.ya[:, 64 * h:64 * h + 64, :]).then_inc(T.sem.fin, 16)
-    for h in range(2):
-        Y.wait_ge(T.sem["ar%d" % (4 + h)], come)
-        Y.dma_start(T.y[:, SL + 512 * h:SL + 512 * h + 512], T[DST[4 + h]][:]).then_inc(T.sem.fin, 16)
-    Y.wait_ge(T.sem.fin, 64)
+    span = [(PARTS[ps[0]][0], PARTS[ps[-1]][1]) for ps in OUT]
+    for x, ps in enumerate(OUT):
+        for p in ps:
+            wait(Y, "n" + p, WAVES)
+        Y.dma_start(T[SRC[5 + x]][:], T.last[:, span[x][0]:span[x][1]]).then_inc(T.sem["st%d" % (5 + x)], 16)
+    for x in range(len(OUT)):
+        own(5 + x, S)
+    S.wait_ge(T.sem.ar4, come)
+    S.wait_ge(T.sem.snt, len(SRC) * sent)
+    S.dma_start(T.y[:, 0:SL], T.y0[:]).then_inc(T.sem.fin, 16)
+    for x in range(len(OUT)):
+        Y.wait_ge(T.sem["ar%d" % (5 + x)], come)
+        Y.dma_start(T.y[:, SL + span[x][0]:SL + span[x][1]], T[DST[5 + x]][:]).then_inc(T.sem.fin, 16)
+    Y.wait_ge(T.sem.fin, 16 + 16 * len(OUT))
     for name in cnt:
         if seen.get(name, 0) < cnt[name]:
             P.wait_ge(T.sem[name], cnt[name])

from concourse.bass import DstId, RemoteDMATransfer
from concourse.mybir import AluOpType as A, ActivationFunctionType as F

N, SL, WB, CAP, WAVES = 8, 1024, 2048, 160, 4
ZC = 4 * WB
BIG = 2048
HALF = [(sg * WB - ZC) / 2 for sg in range(4)]
PARTS = {"A": (0, 512), "B": (512, 768), "C": (768, 1024)}
LISTS = {"A": (0, 64), "B": (64, 128)}
KIND = [0, 1, 1, 2]
CUTS = [[0, 32, 64, 96, 116, 128], [0, 30, 64, 86, 106, 128], [0, 24, 64, 104, 114, 128]]
OUT = [["A"], ["B"], ["C"]]
BY_DMA_A, BY_DMA_B = [1, 2], [2]
FIRST_DMA = [(0, 0), (2, 1), (2, 0), (1, 0), (1, 1)]
FIRST_PE = [(3, 1, 0), (3, 1, 1), (3, 0, 0), (3, 0, 1)]
ORDER = [{
    "V": "aiA whoA blkA hotA aiB scanA whoB blkfA hotB carry scanB blkB blkfB offA offB g1 g4 g2 nA nC nB".split(),
    "S": "shl ev0 ev1 cmpA cmpB ev2 ev3 g0 g3 qA qC qB".split(),
    "P": "hs namA namB pr0 pr1 upA cntA pr2 bkA upB finA cntB pr3 bkB finB baseA baseB baseC hA hC hB".split(),
}, {
    "V": "aiA whoA blkA hotA aiB scanA whoB blkfA hotB carry scanB blkB blkfB offA g1 offB g4 g2 nA nC nB".split(),
    "S": "ev0 ev1 cmpA ev2 cmpB g0 g3 qA qC qB".split(),
    "P": "namA pr0 namB pr1 pr2 upA cntA baseB bkA upB finA cntB baseA bkB finB hA baseC hC hB".split(),
}, {
    "V": "aiA whoA blkA hotA aiB scanA whoB blkfA hotB carry scanB blkB offA blkfB g1 offB g2 nA nB nC".split(),
    "S": "ev0 ev1 cmpA ev2 cmpB g0 qA g3 g4 qB qC".split(),
    "P": "namA pr0 namB pr1 pr2 upA cntA baseB bkA finA upB cntB baseA bkB finB hA baseC hB hC".split(),
}]

SCRATCH = {
    "dk": ("dram", [128, 1], "bfloat16"), "lk": ("dram", [8, 128, 1], "bfloat16"),
    "dg": ("dram", [8, 128, 32], "bfloat16"), "lg": ("dram", [8, 128, 32], "bfloat16"),
    "d1": ("dram", [8, 128, 128], "bfloat16"), "l1": ("dram", [8, 128, 128], "bfloat16"),
    "d0": ("dram", [8, 128, 128], "bfloat16"), "l0": ("dram", [8, 128, 128], "bfloat16"),
    "e0": ("dram", [8, 128, 128], "bfloat16"), "y0": ("dram", [8, 128, 128], "bfloat16"),
    "win": ("sbuf", [128, ZC + 16], "bfloat16"),
    "ref": ("sbuf", [128, 2048], "bfloat16"),
    "tq": ("sbuf", [128, SL], "bfloat16"), "last": ("sbuf", [128, SL], "bfloat16"),
    "off": ("sbuf", [128, 128], "uint16"),
    "ai": ("sbuf", [128, 128], "int32"), "who": ("sbuf", [128, 128], "int32"), "blk": ("sbuf", [128, 128], "int32"),
    "blkf": ("sbuf", [128, 128], "float32"),
    "hotA": ("sbuf", [128, 256], "bfloat16"), "runA": ("sbuf", [128, 256], "bfloat16"), "keepA": ("sbuf", [128, 256], "bfloat16"),
    "hotB": ("sbuf", [128, 260], "bfloat16"), "runB": ("sbuf", [128, 260], "bfloat16"), "keepB": ("sbuf", [128, 260], "bfloat16"),
    "okA": ("sbuf", [128, 256], "bfloat16"), "okB": ("sbuf", [128, 256], "bfloat16"),
    "ones": ("sbuf", [128, 512], "bfloat16"),
    "jj": ("sbuf", [128, 128], "int32"), "pp": ("sbuf", [128, 8], "int32"),
    "ti": ("sbuf", [128, 384], "int32"), "tk": ("sbuf", [128, 256], "float32"),
    "ci": ("sbuf", [128, 16], "int32"), "cf": ("sbuf", [128, 16], "float32"), "cg": ("sbuf", [128, 8], "float32"),
    "sli": ("sbuf", [128, 8], "int32"), "slf": ("sbuf", [128, 4], "float32"), "grp": ("sbuf", [128, 8], "float32"),
    "id2": ("sbuf", [128, 256], "bfloat16"), "idf": ("sbuf", [128, 128], "float32"),
    "coef": ("sbuf", [128, 512], "bfloat16"), "one8": ("sbuf", [128, 128], "bfloat16"),
    "low": ("sbuf", [128, 256], "bfloat16"), "upp": ("sbuf", [128, 128], "bfloat16"), "swp": ("sbuf", [128, 128], "bfloat16"),
    "msk": ("sbuf", [128, 1024], "bfloat16"), "lw": ("sbuf", [128, 1024], "bfloat16"), "c258": ("sbuf", [128, 128], "bfloat16"),
    "wc": ("sbuf", [128, 16], "bfloat16"), "gcb": ("sbuf", [128, 16], "bfloat16"), "hc": ("sbuf", [128, 16], "bfloat16"),
    "gbd": ("sbuf", [128, 128], "bfloat16"), "hb": ("sbuf", [128, 256], "bfloat16"), "hl": ("sbuf", [128, 256], "bfloat16"),
    "vA": ("psum", [128, 512], "float32"), "vB": ("psum", [128, 512], "float32"), "vC": ("psum", [128, 512], "float32"),
    "bA": ("psum", [128, 512], "float32"), "bB": ("psum", [128, 512], "float32"), "pf": ("psum", [128, 512], "float32"),
    "r0": ("psum", [128, 512], "float32"), "r1": ("psum", [128, 512], "float32"),
}
SRC = ["dk", "dg", "d1", "d0", "e0"]
DST = ["lk", "lg", "l1", "l0", "y0"]
STAGED = [16, 32, 16, 16, 16]
for x, ps in enumerate(OUT):
    width = (PARTS[ps[-1]][1] - PARTS[ps[0]][0]) // 8
    SCRATCH["e%d" % (x + 1)] = ("dram", [8, 128, width], "bfloat16")
    SCRATCH["y%d" % (x + 1)] = ("dram", [8, 128, width], "bfloat16")
    SRC.append("e%d" % (x + 1))
    DST.append("y%d" % (x + 1))
    STAGED.append(16)
SEMAPHORES = (["iot", "cv", "snt", "ldw", "ldg", "ldx1", "ldx0", "rep", "slw", "bdv", "bds", "fin"]
              + sorted(set(sum(ORDER[0].values(), []) + ["ev4", "ev5", "pr4", "pr5"]))
              + ["st%d" % i for i in range(len(SRC))] + ["ar%d" % i for i in range(len(SRC))])


def bits(engines):
    m = 0
    for e in engines:
        m |= 1 << e
    return m


def routes(T, topo, r):
    src = T.cores[r]
    near = [q for q in range(N) if q != r and topo.may_write(src, T.cores[q])]
    far = [q for q in range(N) if q != r and q not in near]
    able = [h for h in topo.cores_of(src) if h != src and all(topo.may_write(h, T.cores[q]) for q in far)]
    able.sort(key=lambda h: (topo.die(h) == topo.die(src), h))
    me = sorted(near + [r]).index(r)
    return near, [(able[(me + b) % len(able)], q) for b, q in enumerate(far)], able


def helper_program(g, core, T, topo):
    for r in range(N):
        near, far, able = routes(T, topo, r)
        for h, q in far:
            if h != core:
                continue
            dst = T.cores[q]
            rid, pid = topo.addr(dst, core)
            eng = topo.engines(core, dst)[0::2]
            for k in range(len(DST)):
                g.wait_ge(T.sem["ar%d" % k], 2)
                g.remote_dma(T[DST[k]][r], T[DST[k]][0], T.sem["ar%d" % k], T.sem.snt, pid, rid, bits(eng))
            g.wait_ge(T.sem.snt, len(DST) * len(eng))


def rank_program(g, core, T, topo):
    me = T.rank_of(core)
    if me is None:
        helper_program(g, core, T, topo)
        return
    V, P, S, Y = g.vector, g.tensor, g.scalar, g.sync
    cnt, seen = {}, {}

    def inc(ins, name, n=1):
        ins.then_inc(T.sem[name], n)
        cnt[name] = cnt.get(name, 0) + n

    def wait(q, name, n):
        q.wait_ge(T.sem[name], n)
        seen[name] = max(seen.get(name, 0), n)

    near, far, able = routes(T, topo, me)
    off_eng = topo.engines(core, T.cores[near[0]])
    on_eng = [e for e in topo.engines(core, able[0]) if e not in off_eng]
    hmask = {}
    for x, h in enumerate(able):
        b = 4 * (x % 2) + x // 2
        hmask[h] = bits([on_eng[b], on_eng[b + 2]])
    sent = len(near) + 2 * len(far)
    come = 16 + len(near) + len(far) * len(off_eng[0::2])

    def piece(k, q):
        return T.dk[:] if k == 0 else T[SRC[k]][q]

    def send(k):
        out = []
        for h, q in far:
            rid, pid = topo.addr(h, core)
            out.append(RemoteDMATransfer(dst_ids=[DstId(rid=rid, pnc=pid)], dma_engine_mask=hmask[h],
                                         remote_sem=T.sem["ar%d" % k], src=piece(k, q), dst=T[DST[k]][0]))
        for x, q in enumerate(near):
            rid, pid = topo.addr(T.cores[q], core)
            out.append(RemoteDMATransfer(dst_ids=[DstId(rid=rid, pnc=pid)], dma_engine_mask=bits([off_eng[2 * x]]),
                                         remote_sem=T.sem["ar%d" % k], src=piece(k, q), dst=T[DST[k]][me]))
        g.remote_dma_fused(out, local_sem=T.sem.snt)

    def own(k, q=Y):
        q.wait_ge(T.sem["st%d" % k], STAGED[k])
        q.dma_start(T[DST[k]][me], piece(k, me)).then_inc(T.sem["ar%d" % k], 16)

    W = T.win

    def cols(sg, s, a=0, b=SL):
        return slice(sg * WB + s * SL + a, sg * WB + s * SL + b)

    Y.dma_start(T.dk[:], T.kw[:]).then_inc(T.sem.st0, 16)
    S.dma_start(T.dg[:, 0:64, :], T.gm[:]).then_inc(T.sem.st1, 16)
    Y.dma_start(T.dg[:, 64:128, :], T.hm[:]).then_inc(T.sem.st1, 16)
    S.dma_start(T.d1[:], T.m[:, SL:WB]).then_inc(T.sem.st2, 16)
    Y.dma_start(T.d0[:], T.m[:, 0:SL]).then_inc(T.sem.st3, 16)

    inc(g.iota(T.jj[:], [[1, 128]], 0, 0), "iot")
    inc(g.iota(T.pp[:], [[0, 8]], 0, 1), "iot")
    for k, n in enumerate(STAGED):
        g.wait_ge(T.sem["st%d" % k], n)
        send(k)
    g.wait_ge(T.sem.snt, len(SRC) * sent)

    def level():
        wait(V, "cv", cnt["cv"])

    def ts(out, in0, s1, op0, s2=None, op1=None):
        if op1 is None:
            return V.tensor_scalar(out, in0, s1, None, op0)
        return V.tensor_scalar(out, in0, s1, s2, op0, op1)

    inc(V.memset(T.ones[:], 1.0), "cv")
    inc(V.memset(T.keepA[:], 1.0), "cv")
    inc(V.memset(T.keepB[:], 1.0), "cv")
    inc(V.memset(T.c258[:], 258.0), "cv")
    inc(V.memset(T.hb[:], 0.0), "cv")
    inc(V.memset(W[:, ZC:ZC + 16], 0.0), "cv")
    wait(V, "iot", 2)
    sr, an = A.logical_shift_right, A.bitwise_and
    J, pc0 = T.jj, T.pp[:, 0:1]
    inc(ts(T.ti[:, 0:128], J[:], 0x71, an), "cv")
    inc(ts(T.ti[:, 128:256], J[:], 5, sr), "cv")
    inc(ts(T.ti[:, 256:384], J[:], 15, an), "cv")
    inc(V.tensor_copy(T.ci[:, 0:1], pc0), "cv")
    inc(ts(T.ci[:, 1:2], pc0, 0x71, an), "cv")
    inc(ts(T.ci[:, 2:3], pc0, 4, sr), "cv")
    inc(ts(T.ci[:, 3:4], pc0, 5, sr), "cv")
    inc(ts(T.ci[:, 4:5], pc0, 15, an), "cv")
    inc(ts(T.ci[:, 5:6], pc0, 4, sr, 1, an), "cv")
    inc(ts(T.ci[:, 6:7], pc0, 1, an), "cv")
    level()
    inc(V.tensor_copy(T.cf[:, 0:7], T.ci[:, 0:7]), "cv")
    inc(ts(T.tk[:, 0:128], T.ti[:, 128:256], 16.0, A.mult), "cv")
    level()
    cf = T.cf
    inc(V.tensor_tensor(T.tk[:, 128:256], T.tk[:, 0:128], T.ti[:, 256:384], A.add), "cv")
    inc(ts(T.cg[:, 0:1], cf[:, 3:4], 16.0, A.mult, cf[:, 4:5], A.add), "cv")
    inc(ts(T.cg[:, 2:3], cf[:, 3:4], 16.0, A.mult, cf[:, 5:6], A.add), "cv")
    inc(V.tensor_tensor(T.cg[:, 3:4], cf[:, 5:6], cf[:, 6:7], A.not_equal), "cv")
    inc(ts(T.sli[:, 0:4], J[:, 0:4], 2.0, A.mult, cf[:, 2:3], A.add), "cv")
    inc(ts(T.grp[:], J[:, 0:8], cf[:, 2:3], A.is_equal), "cv")
    inc(ts(T.id2[:, 0:128], J[:], cf[:, 0:1], A.is_equal), "cv")
    inc(ts(T.id2[:, 128:256], J[:], cf[:, 0:1], A.is_equal), "cv")
    inc(ts(T.idf[:], J[:], cf[:, 0:1], A.is_equal), "cv")
    for sg in range(4):
        inc(ts(T.coef[:, 128 * sg:128 * sg + 128], J[:], cf[:, 0:1], A.is_equal, HALF[sg], A.mult), "cv")
    inc(ts(T.one8[:], T.ti[:, 0:128], cf[:, 1:2], A.is_equal), "cv")
    inc(ts(T.low[:, 0:128], J[:], cf[:, 0:1], A.is_lt, -1.0, A.mult), "cv")
    level()
    inc(ts(T.sli[:, 4:8], T.sli[:, 0:4], 7, an), "cv")
    inc(V.tensor_tensor(T.low[:, 128:256], T.low[:, 0:128], T.one8[:], A.mult), "cv")
    inc(ts(T.swp[:], T.tk[:, 128:256], T.cg[:, 0:1], A.is_equal), "cv")
    inc(ts(T.keepA[:, 0:64], T.ones[:, 0:64], T.cg[:, 3:4], A.mult), "cv")
    inc(ts(T.keepB[:, 0:65], T.ones[:, 0:65], T.cg[:, 3:4], A.mult), "cv")
    level()
    inc(V.tensor_copy(T.slf[:], T.sli[:, 4:8]), "cv")
    inc(V.tensor_tensor(T.upp[:], T.low[:, 128:256], T.coef[:, 256:384], A.add), "cv")
    inc(V.memset(T.keepA[:, 0:256:64], 0.0), "cv")
    inc(V.memset(T.keepB[:, 0:260:65], 0.0), "cv")
    for e in range(8):
        inc(ts(T.msk[:, 128 * e:128 * e + 128], T.tk[:, 128:256], 2.0 * e, A.subtract, T.cg[:, 2:3], A.is_equal), "cv")
    level()
    consts = cnt["cv"]
    wait(V, "ldw", 16)
    inc(ts(T.lw[:], T.msk[:], T.wc[:, 0:1], A.mult), "slw")

    for k in range(4):
        own(k)
    S.wait_ge(T.sem.ar0, come)
    inc(S.dma_start(T.wc[:, 0:1], T.lk[:, 16 * me:16 * me + 16, 0]), "ldw", 16)
    S.wait_ge(T.sem.ar1, come)
    row, c0 = me // 2, (16 * me) % 32
    inc(S.dma_start(T.hc[:], T.lg[:, 64 + row:128:4, c0:c0 + 16]), "ldg", 16)
    inc(S.dma_start(T.gcb[:], T.lg[:, row:64:4, c0:c0 + 16]), "ldg", 16)
    wait(S, "cv", consts)
    wait(S, "ldg", 32)
    for r in range(8):
        a = 128 * (r % 2) + 16 * r
        inc(S.activation(T.hb[:, a:a + 16], T.hc[:], F.Copy, scale=T.grp[:, r:r + 1]), "bds")
    wait(V, "ldg", 32)
    for r in range(8):
        inc(ts(T.gbd[:, 16 * r:16 * r + 16], T.gcb[:], T.grp[:, r:r + 1], A.mult), "bdv")
    wait(P, "cv", consts)

    def turned(sg, dst, src):
        inc(Y.dma_start(W[0:128 - 32 * sg, dst], src(32 * sg, 128)), "rep", 16)
        inc(Y.dma_start(W[128 - 32 * sg:128, dst], src(0, 32 * sg)), "rep", 16)

    land = [T.l0, T.l1]
    Y.wait_ge(T.sem.ar2, come)
    inc(Y.dma_start(W[:, cols(0, 1)], T.l1[:]), "ldx1", 16)
    here = [False, True]
    for sg, s in FIRST_DMA:
        if not here[s]:
            Y.wait_ge(T.sem.ar3, come)
            here[s] = True
        if sg == 0:
            inc(Y.dma_start(W[:, cols(0, s)], land[s][:]), "ldx0", 16)
        else:
            turned(sg, cols(sg, s), lambda a, b: land[s][a // 16:b // 16])

    ident = T.id2[:, 0:128]
    queue = {"V": V, "S": S, "P": P}
    total = {}

    def order(q, t):
        return ORDER[KIND[t]][q]

    def copy(name, t, out, src):
        return [V.tensor_copy(out, src) if name in order("V", t) else S.activation(out, src, F.Copy)]

    def steps(t):
        s, sp = t % 2, (t + 1) % 2
        st = {}
        cut = CUTS[KIND[t]]
        gathers = {"g%d" % x: (cut[x], cut[x + 1]) for x in range(len(cut) - 1)}

        def made(parts):
            return [("n" + x, t - 1) for x in parts] if t else [("ldx1", None)]

        def into(x):
            a, b = PARTS[x]
            return T.last[:, a:b] if t + 1 == WAVES else W[:, cols(0, s, a, b)]

        if t == 0:
            jobs = [(sg, sl, h, [("ldx%d" % sl, None)]) for sg, sl, h in FIRST_PE]
            st["hs"] = ([("bds", None)], 1, lambda: [P.matmul(T.pf[:, 0:256], T.swp[:], T.hb[:], True, True)])
            st["shl"] = ([("hs", 0)], 1, lambda: [S.activation(T.hl[:], T.pf[:, 0:256], F.Copy)])
        else:
            jobs = ([(sg, sp, 0, made("A")) for sg in (1, 2, 3) if sg not in BY_DMA_A]
                    + [(sg, sp, 1, made("BC")) for sg in (1, 2, 3) if sg not in BY_DMA_B])
        for x, (sg, sl, h, dep) in enumerate(jobs):
            bank = [T.r0, T.r1][x % 2]
            st["pr%d" % x] = (dep + ([("ev%d" % (x - 2), t)] if x > 1 else []), 1, lambda sg=sg, sl=sl, h=h, bank=bank: [
                P.matmul(bank[:], T.id2[:, 32 * sg:32 * sg + 128], W[:, cols(0, sl, 512 * h, 512 * h + 512)], True, True)])
            st["ev%d" % x] = ([("pr%d" % x, t)], 1, lambda x=x, sg=sg, sl=sl, h=h, bank=bank: copy(
                "ev%d" % x, t, W[:, cols(sg, sl, 512 * h, 512 * h + 512)], bank[:]))
        window = [("rep", None)] + [("ev%d" % x, t) for x in range(len(jobs))]

        for x, (k0, k1) in LISTS.items():
            k, bank, lead = slice(k0, k1), T["b" + x], int(x == "B")
            hot, run, ok, w = T["hot" + x], T["run" + x], T["ok" + x], 64 + lead

            def named(k0=k0, k1=k1, bank=bank):
                for e in range(8):
                    a = sp * SL
                    mm = P.matmul(bank[:, 0:64], T.lw[:, 128 * e:128 * e + 128], W[:, a + 8 * k0 + e:a + 8 * k1:8], e == 0, e == 7)
                return [mm]

            def count(lhs, src, first, bank=bank, lead=lead, w=w):
                if lead:
                    for sg in range(4):
                        mm = P.matmul(bank[:, 64 + 64 * sg:128 + 64 * sg], lhs, src[:, w * sg + 1:w * sg + w],
                                      first and sg == 0, not first and sg == 3)
                else:
                    mm = P.matmul(bank[:, 64:320], lhs, src[:], first, not first)
                return [] if first else [mm]

            def block(k=k):
                P.matmul(T.pf[:, k], T.idf[:], T.blkf[:, k], True, False)
                return []

            def final(k=k, ok=ok):
                for sg in range(4):
                    mm = P.matmul(T.pf[:, k], T.coef[:, 128 * sg:128 * sg + 128], ok[:, 64 * sg:64 * sg + 64], False, sg == 3)
                return [mm]

            on_s = "cmp" + x in order("S", t)
            st["nam" + x] = (made("A" if x == "A" else "BC") + ([("slw", None)] if t == 0 else []), 1, named)
            st["ai" + x] = ([("nam" + x, t)], 1, lambda k=k, bank=bank: [V.tensor_copy(T.ai[:, k], bank[:, 0:64])])
            st["who" + x] = ([("ai" + x, t)], 1, lambda k=k: [ts(T.who[:, k], T.ai[:, k], N - 1, an)])
            st["blk" + x] = ([("ai" + x, t)], 1, lambda k=k: [ts(T.blk[:, k], T.ai[:, k], 3, sr, WB - 1, an)])
            st["blkf" + x] = ([("blk" + x, t)], 1, lambda k=k: [V.tensor_copy(T.blkf[:, k], T.blk[:, k])])
            st["hot" + x] = ([("who" + x, t)], 4, lambda k=k, hot=hot, lead=lead, w=w: [
                ts(hot[:, w * sg + lead:w * sg + w], T.who[:, k], T.slf[:, sg:sg + 1], A.is_equal) for sg in range(4)])
            st["scan" + x] = ([("hot" + x, t)] + [("carry", t)] * lead, 1, lambda x=x, hot=hot, run=run: [
                V.tensor_tensor_scan(run[:], T["keep" + x][:], hot[:], 0.0, A.mult, A.add)])
            st["up" + x] = ([("hot" + x, t)] + [("carry", t)] * lead, 0, lambda count=count, hot=hot: count(T.upp[:], hot, True))
            st["cnt" + x] = ([("scan" + x, t)], 1, lambda count=count, run=run: count(T.one8[:], run, False))
            st["cmp" + x] = ([("cnt" + x, t)], 1, lambda bank=bank, ok=ok, on_s=on_s: [
                S.activation(ok[:], bank[:, 64:320], F.Sign, bias=CAP - BIG + 0.5, scale=-1.0) if on_s else
                ts(ok[:], bank[:, 64:320], float(CAP - BIG), A.is_le, 2.0, A.mult)])
            st["bk" + x] = ([("blkf" + x, t)] + ([("offA", t)] if lead else [("shl", 0)] * (t == 0)), 0, block)
            st["fin" + x] = ([("cmp" + x, t)], 1, final)
            st["off" + x] = ([("fin" + x, t)], 1, lambda k=k, on_s=on_s: [
                ts(T.off[:, k], T.pf[:, k], ZC + sum(HALF) * on_s, A.add, float(ZC), A.min)])
        st["carry"] = ([("scanA", t)], 1, lambda: copy("carry", t, T.hotB[:, 0:260:65], T.runA[:, 63:256:64]))

        for x, (k0, k1) in gathers.items():
            st[x] = (window + [("offA", t)] * (k0 < 64) + [("offB", t)] * (k1 > 64), 1, lambda x=x, k0=k0, k1=k1: copy(
                x, t, T.ref[:, 16 * k0:16 * k1], W[:, 0:ZC + 16].indirect(T.off[:, k0:k1])))

        for x, (a, b) in PARTS.items():
            bank, n = T["v" + x], b - a

            def base(a=a, b=b, bank=bank, n=n):
                P.matmul(bank[:, 0:n], T.c258[:], T.ones[:, 0:n], True, False)
                P.matmul(bank[:, 0:n], ident, W[:, cols(0, s, a, b)], False, False)
                P.matmul(bank[:, 0:n], T.gbd[:], W[:, cols(0, sp, a, b)], False, False)
                return []

            def href(a=a, b=b, bank=bank, n=n):
                for q in range(2):
                    mm = P.matmul(bank[:, 0:n], T.hl[:, 128 * q:128 * q + 128], T.ref[:, 2 * a + q:2 * b:2], False, q == 1)
                return [mm]

            def quot(x=x, a=a, b=b, bank=bank, n=n):
                if "q" + x in order("V", t):
                    return [ts(T.tq[:, a:b], bank[:, 0:n], -127.5, A.add)]
                return [S.activation(T.tq[:, a:b], bank[:, 0:n], F.Identity, bias=-127.5)]

            st["base" + x] = (made(x) + ([("ldx0", None), ("bdv", None)] if t == 0 else []), 0, base)
            st["h" + x] = ([(y, t) for y, (k0, k1) in gathers.items() if 8 * k0 < b and 8 * k1 > a], 1, href)
            st["q" + x] = ([("h" + x, t)], 1, quot)
            st["n" + x] = ([("q" + x, t)] + [(y, t) for y in gathers if t + 1 < WAVES], 1, lambda x=x, a=a, b=b, bank=bank, n=n: [
                V.tensor_tensor(into(x), bank[:, 0:n], T.tq[:, a:b], A.subtract)])
        return st

    passed = {q: {} for q in queue}
    for t in range(WAVES):
        st, sp = steps(t), (t + 1) % 2
        for name, (dep, n, calls) in st.items():
            total[name, t] = cnt.get(name, 0) + n
        if t > 0:
            for parts, h, slots in (("A", 0, BY_DMA_A), ("BC", 1, BY_DMA_B)):
                for x in parts:
                    wait(Y, "n" + x, total["n" + x, t - 1])
                for sg in slots:
                    turned(sg, cols(sg, sp, 512 * h, 512 * h + 512), lambda a, b: W[a:b, cols(0, sp, 512 * h, 512 * h + 512)])
        if t + 1 == WAVES:
            Y.dma_start(T.e0[:], W[:, cols(0, 0)]).then_inc(T.sem.st4, 16)
            own(4)
        for q in queue:
            for name in order(q, t):
                if name not in st:
                    continue
                dep, n, calls = st[name]
                for d, u in dep:
                    need = cnt[d] if u is None else total[d, u]
                    if passed[q].get(d, 0) < need:
                        wait(queue[q], d, need)
                        passed[q][d] = need
                for ins in calls():
                    inc(ins, name)

    span = [(PARTS[ps[0]][0], PARTS[ps[-1]][1]) for ps in OUT]
    for x, ps in enumerate(OUT):
        for p in ps:
            wait(Y, "n" + p, WAVES)
        Y.dma_start(T[SRC[5 + x]][:], T.last[:, span[x][0]:span[x][1]]).then_inc(T.sem["st%d" % (5 + x)], 16)
    for x in range(len(OUT)):
        own(5 + x, S)
    S.wait_ge(T.sem.ar4, come)
    S.wait_ge(T.sem.snt, len(SRC) * sent)
    S.dma_start(T.y[:, 0:SL], T.y0[:]).then_inc(T.sem.fin, 16)
    for x in range(len(OUT)):
        Y.wait_ge(T.sem["ar%d" % (5 + x)], come)
        Y.dma_start(T.y[:, SL + span[x][0]:SL + span[x][1]], T[DST[5 + x]][:]).then_inc(T.sem.fin, 16)
    Y.wait_ge(T.sem.fin, 16 + 16 * len(OUT))
    for name in cnt:
        if seen.get(name, 0) < cnt[name]:
            P.wait_ge(T.sem[name], cnt[name])
